import numpy as np
import ml_dtypes


def mxq(x, axis, fmt="e4m3"):
    dtype, down = {"e4m3": (ml_dtypes.float8_e4m3fn, 7), "e5m2": (ml_dtypes.float8_e5m2, 14)}[fmt]
    v = np.moveaxis(np.asarray(x, np.float32).astype(ml_dtypes.bfloat16).astype(np.float64), axis, -1)
    blocks = v.reshape(v.shape[:-1] + (-1, 32))
    amax = np.abs(blocks).max(-1, keepdims=True)
    byte = np.maximum(np.where(amax > 0, np.frexp(amax)[1] - 1 + 127, 0) - down, 1)
    scale = np.exp2(byte - 127.0)
    codes = (blocks / scale).astype(np.float32).astype(dtype).astype(np.float64)
    return np.moveaxis((codes * scale).reshape(v.shape), -1, axis)


WIDE = False


def mx_kscale(k):
    if not WIDE:
        return np.ones(k)
    levels = np.array([10, -10, 5, -5, 0])
    if k % 512:
        return np.exp2(np.random.permutation(np.resize(levels, k // 32))).repeat(32)
    a = np.empty((k // 512, 16))
    for p in range(k // 512):
        a[p, :8] = np.random.permutation(np.resize(levels, 8))
        for g in range(8):
            far = levels[np.abs(levels - a[p, g]) >= 10]
            a[p, g + 8] = far[np.random.randint(len(far))]
    return np.exp2(a.ravel()).repeat(32)


def f64(x):
    return np.asarray(x).astype(np.float64)


def striped(idx):
    return np.tile(idx.reshape(-1, 16).T, (8, 1)).astype(np.uint16)


def unstriped(offs):
    return offs[:16].T.reshape(-1).astype(np.int64)


def pack_weight(w):
    k, n = w.shape
    w = f64(np.asarray(w, np.float32).astype(ml_dtypes.bfloat16)).reshape(k // 32, 32, n)
    amax = np.abs(w).max(1)
    byte = np.clip(np.where(amax > 0, np.frexp(amax)[1] - 1 + 127 - 7, 1), 1, 254)
    scaled = (w * np.exp2(127.0 - byte)[:, None, :]).reshape(k, n).astype(np.float32)
    words = np.ascontiguousarray(scaled.reshape(k // 512, 128, 4, n).transpose(0, 1, 3, 2)).astype(ml_dtypes.float8_e4m3fn).view(np.uint8)
    return words, np.ascontiguousarray(byte.astype(np.uint8).reshape(k // 512, 16, n))


def unpack_weight(words, scales):
    g, p, n, _ = words.shape
    vals = np.ascontiguousarray(words).view(ml_dtypes.float8_e4m3fn).astype(np.float64) * np.repeat(np.exp2(scales.astype(np.float64) - 127.0), 8, axis=1)[..., None]
    return vals.transpose(0, 1, 3, 2).reshape(g * 512, n)


E2M1 = np.array([0.0, 0.5, 1.0, 1.5, 2.0, 3.0, 4.0, 6.0, -0.0, -0.5, -1.0, -1.5, -2.0, -3.0, -4.0, -6.0])


def pack_fp4(w):
    k, n = w.shape
    w = f64(np.asarray(w, np.float32).astype(ml_dtypes.bfloat16)).reshape(k // 32, 32, n)
    amax = np.abs(w).max(1)
    mant, ex = np.frexp(amax / 6.0)
    byte = np.clip(np.where(amax > 0, np.where(mant > 0.5, ex, ex - 1) + 127, 1), 1, 254)
    scaled = (w * np.exp2(127.0 - byte)[:, None, :]).reshape(k, n).astype(np.float32)
    c = np.ascontiguousarray(scaled.reshape(k // 512, 128, 4, n).transpose(0, 1, 3, 2)).astype(ml_dtypes.float4_e2m1fn).view(np.uint8) & 0xF
    words = (c[..., 0::2] | (c[..., 1::2] << 4)).reshape(k // 512, 128, 2 * n)
    return np.ascontiguousarray(words), np.ascontiguousarray(byte.astype(np.uint8).reshape(k // 512, 16, n))


def unpack_fp4(words, scales):
    g, _, n = scales.shape
    words = np.ascontiguousarray(words).reshape(g, 128, n, 2)
    nib = np.empty((g, 128, n, 4), np.uint8)
    nib[..., 0::2] = words & 0xF
    nib[..., 1::2] = words >> 4
    vals = E2M1[nib] * np.repeat(np.exp2(scales.astype(np.float64) - 127.0), 8, axis=1)[..., None]
    return vals.transpose(0, 1, 3, 2).reshape(g * 512, n)


def sigmoid(v):
    return 1.0 / (1.0 + np.exp(-np.maximum(v, -700.0)))


K, T, S, D, N, H, V, U = 1024, 2048, 1024, 4, 256, 512, 256, 512


def setup_inputs():
    n = np.random.standard_normal
    s = mx_kscale(K)[:, None]
    u = mx_kscale(H)
    packed_xT = pack_weight(n((K, T)) * s)
    packed_w1 = pack_fp4(n((K, H)) / np.sqrt(K) / s)
    packed_w2 = pack_fp4(n((H, N)) / np.sqrt(H) / u[:, None])
    return {
        "x_words": packed_xT[0],
        "x_scales": packed_xT[1],
        "w1_words": packed_w1[0],
        "w1_scales": packed_w1[1],
        "thr": (np.random.uniform(-0.3, 0.8, (H, U))).astype(np.float32),
        "unit": (np.random.uniform(0.6, 1.4, (H, 1)) * u[:, None]).astype(np.float32),
        "w2_words": packed_w2[0],
        "w2_scales": packed_w2[1],
        "offs": striped(np.random.permutation(T)[:S]),
        "slot": striped(np.random.permutation(np.concatenate([np.arange(V), np.random.randint(0, V, U - V)]))),
    }


def reference(x_words, x_scales, w1_words, w1_scales, thr, unit, w2_words, w2_scales, offs, slot):
    xq = unpack_weight(x_words, x_scales)[:, unstriped(offs)]
    y = unpack_fp4(w1_words, w1_scales).T @ xq
    prtop = y.reshape(len(y), -1, D).max(axis=2)
    prexp = np.exp(y - np.repeat(prtop, D, axis=1))
    prsum = prexp.reshape(len(prexp), -1, D).sum(axis=2)
    pr = prexp / np.repeat(prsum, D, axis=1)
    py = pr * y
    ev = py.reshape(len(py), -1, D).sum(axis=2)
    cs = ev[:, unstriped(slot)]
    kp = sigmoid(2.0 * (cs - f64(thr)))
    best = y.reshape(len(y), -1, D).max(axis=2)
    hid = f64(unit) * (kp * (best[:, unstriped(slot)] - ev[:, unstriped(slot)]))
    return unpack_fp4(w2_words, w2_scales).T @ mxq(hid, 0, "e4m3")

@@ -1,0 +1,233 @@
+from contextlib import ExitStack
+
+import concourse.mybir as mybir
+from concourse.masks import make_identity
+
+K, T, S, D, N, H, V, U = 1024, 2048, 1024, 4, 256, 512, 256, 512
+FLOPS = 2 * K * H * S + 2 * H * N * U
+
+F32 = mybir.dt.float32
+BF16 = mybir.dt.bfloat16
+I32 = mybir.dt.int32
+U32 = mybir.dt.uint32
+U16 = mybir.dt.uint16
+U8 = mybir.dt.uint8
+FP8X4 = mybir.dt.float8_e4m3fn_x4
+FP4X4 = mybir.dt.float4_e2m1fn_x4
+ALU = mybir.AluOpType
+ACT = mybir.ActivationFunctionType
+AX = mybir.AxisListType
+
+P = 128
+PASSES = K // 512
+QUARTERS = H // P
+HALF = 512
+WINDOW = V + 16
+GUESS_SLOPE, GUESS_SHIFT, GUESS_FLOOR = -0.9609375, 0.6875, 0.2135
+
+
+def tile_picked_ymaskd_gap_p_kernel(
+    tc, x_words, x_scales, w1_words, w1_scales, thr, unit, w2_words, w2_scales, offs, slot, out
+):
+    nc = tc.nc
+    with ExitStack() as ctx:
+        keep = ctx.enter_context(tc.tile_pool(name="keep", bufs=1))
+        ring = ctx.enter_context(tc.tile_pool(name="ring", bufs=3))
+        ps_y = ctx.enter_context(tc.psum_pool(name="ps_y", bufs=3))
+        ps_sum = ctx.enter_context(tc.psum_pool(name="ps_sum", bufs=1))
+        ps_turn = ctx.enter_context(tc.psum_pool(name="ps_turn", bufs=3))
+
+        offs_sb = keep.tile([P, S // 16], U16, name="offs_sb")
+        nc.sync.dma_start(offs_sb[:], offs)
+
+        xs = keep.tile([P, T], U8, name="xs", align_bytes=64)
+        nc.vector.memset(xs[:].bitcast(I32), 0)
+        for quad in range(4):
+            nc.sync.dma_start(
+                xs[32 * quad : 32 * quad + 8, :].bitcast(I32),
+                x_scales[:, 4 * quad : 4 * quad + 4, :].bitcast(I32),
+            )
+        xw = [keep.tile([P, T], U32, name="xw%d" % o, align_bytes=64) for o in range(PASSES)]
+        w1w = keep.tile([P, PASSES, 2 * H], U8, name="w1w", align_bytes=64)
+        nc.sync.dma_start(xw[0][:].bitcast(I32), x_words[0].rearrange("p n t -> p (n t)").bitcast(I32))
+        nc.sync.dma_start(w1w[:].bitcast(I32), w1_words.rearrange("o p c -> p o c").bitcast(I32))
+        nc.sync.dma_start(xw[1][:].bitcast(I32), x_words[1].rearrange("p n t -> p (n t)").bitcast(I32))
+
+        w1s = keep.tile([P, PASSES, H], U8, name="w1s", align_bytes=64)
+        nc.gpsimd.memset(w1s[:].bitcast(I32), 0)
+        for quad in range(4):
+            nc.gpsimd.dma_start(
+                w1s[32 * quad : 32 * quad + 4, :, :].bitcast(I32),
+                w1_scales[:, 4 * quad : 4 * quad + 4, :].rearrange("o r c -> r o c").bitcast(I32),
+            )
+
+        ident = keep.tile([P, P], F32, name="ident")
+        make_identity(nc, ident[:])
+        consts = keep.tile([P, 3], F32, name="consts")
+        nc.gpsimd.memset(consts[:, 0:1], GUESS_SHIFT)
+        nc.gpsimd.memset(consts[:, 1:2], 1.0)
+        nc.gpsimd.memset(consts[:, 2:3], 0.5)
+
+        slot_sb = keep.tile([P, U // 16], U16, name="slot_sb")
+        nc.sync.dma_start(slot_sb[:], slot)
+        thr_sb = keep.tile([P, QUARTERS, U], F32, name="thr_sb")
+        nc.sync.dma_start(thr_sb[:], thr.rearrange("(q p) r -> p q r", p=P))
+        w2w = keep.tile([P, 2 * N], U8, name="w2w", align_bytes=64)
+        nc.sync.dma_start(w2w[:].bitcast(I32), w2_words[0].bitcast(I32))
+
+        unit_sb = keep.tile([P, QUARTERS], F32, name="unit_sb")
+        with nc.allow_non_contiguous_dma(reason="one value a partition and quarter"):
+            nc.gpsimd.dma_start(unit_sb[:], unit.rearrange("(q p) o -> p (q o)", p=P))
+        half_unit = keep.tile([P, QUARTERS], F32, name="half_unit")
+        nc.gpsimd.tensor_scalar(half_unit[:], unit_sb[:], 0.5, 0.0, ALU.mult, ALU.add)
+
+        w2s = keep.tile([P, N], U8, name="w2s", align_bytes=64)
+        nc.gpsimd.memset(w2s[:].bitcast(I32), 0)
+        for quad in range(4):
+            nc.gpsimd.dma_start(
+                w2s[32 * quad : 32 * quad + 4, :].bitcast(I32),
+                w2_scales[0, 4 * quad : 4 * quad + 4, :].bitcast(I32),
+            )
+
+        neg_ev = [keep.tile([P, WINDOW], F32, name="neg_ev%d" % q) for q in range(QUARTERS)]
+        gap_unit = [keep.tile([P, WINDOW], F32, name="gap_unit%d" % q) for q in range(QUARTERS)]
+        for q in range(QUARTERS):
+            nc.gpsimd.memset(neg_ev[q][:, V:], 0.0)
+            nc.gpsimd.memset(gap_unit[q][:, V:], 0.0)
+
+        gs0 = keep.tile([P, S], U8, name="gs0", align_bytes=64)
+        nc.vector.tensor_copy(gs0[:], xs[:].indirect(offs_sb[:]))
+        gs1 = keep.tile([P, S], U8, name="gs1", align_bytes=64)
+        nc.vector.memset(gs1[:].bitcast(I32), 0)
+        for quad in range(4):
+            nc.scalar.dma_start(
+                gs1[32 * quad : 32 * quad + 4, :].bitcast(I32),
+                gs0[32 * quad + 4 : 32 * quad + 8, :].bitcast(I32),
+            )
+        gs = [gs0, gs1]
+        gw = {}
+        for o in range(PASSES):
+            for h in range(2):
+                gw[o, h] = keep.tile([P, HALF], U32, name="gw%d%d" % (o, h), align_bytes=64)
+                nc.vector.tensor_copy(gw[o, h][:], xw[o][:].indirect(offs_sb[:, 32 * h : 32 * h + 32]))
+
+        hid_t = [keep.tile([P, 2, H], BF16, name="hid_t%d" % rh, align_bytes=64) for rh in range(2)]
+
+        def turn(dst, src, start=True, stop=True):
+            nc.tensor.matmul(dst, src, ident[:], start=start, stop=stop, is_transpose=True)
+
+        for q in range(QUARTERS):
+            best = keep.tile([P, V], F32, name="best%d" % q)
+            sum_e = ps_sum.tile([P, V], F32, name="sum_e")
+            sum_p = ps_sum.tile([P, V], F32, name="sum_p")
+            for h in range(2):
+                y = ps_y.tile([P, HALF], F32, name="y")
+                for o in range(PASSES):
+                    nc.tensor.matmul_mx(
+                        y[:],
+                        lhsT=w1w[:, o, 256 * q : 256 * q + 256].bitcast(FP4X4),
+                        lhsT_scale=w1s[:, o, P * q : P * q + P],
+                        rhs=gw[o, h][:].bitcast(FP8X4),
+                        rhs_scale=gs[o][:, HALF * h : HALF * h + HALF],
+                        start=(o == 0),
+                        stop=(o == PASSES - 1),
+                    )
+                top = best[:, P * h : P * h + P]
+                nc.vector.tensor_reduce(top, y[:].rearrange("p (v d) -> p v d", d=D), AX.X, ALU.max)
+                diff = ring.tile([P, D, P], F32, name="diff")
+                nc.vector.tensor_tensor(
+                    diff[:],
+                    y[:].rearrange("p (v d) -> p d v", d=D),
+                    top.unsqueeze(1).to_broadcast([P, D, P]),
+                    ALU.subtract,
+                )
+                expd = ring.tile([P, D, P], F32, name="expd")
+                nc.scalar.activation(expd[:], diff[:], ACT.Exp)
+                for d in range(D):
+                    turn(sum_e[:, P * h : P * h + P], expd[:, d, :], d == 0, d == D - 1)
+                prod = ring.tile([P, D, P], F32, name="prod")
+                nc.vector.tensor_tensor(prod[:], expd[:], diff[:], ALU.mult)
+                for d in range(D):
+                    turn(sum_p[:, P * h : P * h + P], prod[:, d, :], d == 0, d == D - 1)
+
+            guess = ring.tile([P, V], F32, name="guess")
+            nc.scalar.activation(guess[:], sum_e[:], ACT.Exp, bias=consts[:, 0:1], scale=GUESS_SLOPE)
+            near_one = ring.tile([P, V], F32, name="near_one")
+            nc.vector.scalar_tensor_tensor(near_one[:], guess[:], GUESS_FLOOR, sum_e[:], ALU.add, ALU.mult)
+            err2 = ring.tile([P, V], F32, name="err2")
+            nc.scalar.activation(err2[:], near_one[:], ACT.Square, bias=consts[:, 1:2], scale=-1.0)
+            series = ring.tile([P, V], F32, name="series")
+            nc.scalar.activation(series[:], err2[:], ACT.Square, bias=consts[:, 2:3], scale=1.0)
+            quot0 = ring.tile([P, V], F32, name="quot0")
+            nc.vector.scalar_tensor_tensor(quot0[:], guess[:], GUESS_FLOOR, sum_p[:], ALU.add, ALU.mult)
+            quot1 = ring.tile([P, V], F32, name="quot1")
+            nc.vector.scalar_tensor_tensor(quot1[:], near_one[:], -2.0, quot0[:], ALU.add, ALU.mult)
+            gap_t = ring.tile([P, V], F32, name="gap_t")
+            nc.vector.scalar_tensor_tensor(gap_t[:], series[:], 0.75, quot1[:], ALU.add, ALU.mult)
+
+            gap = ps_turn.tile([P, HALF], F32, name="turned")
+            for h in range(2):
+                turn(gap[:, P * h : P * h + P], gap_t[:, P * h : P * h + P])
+            nc.vector.tensor_tensor(neg_ev[q][:, :V], gap[:, :V], best[:], ALU.subtract)
+            nc.scalar.activation(gap_unit[q][:, :V], gap[:, :V], ACT.Copy, scale=half_unit[:, q : q + 1])
+
+        for q in range(QUARTERS):
+            for rh in range(2):
+                picks = slot_sb[:, 16 * rh : 16 * rh + 16]
+                ev_slot = ring.tile([P, 256], F32, name="ev_slot")
+                nc.scalar.activation(ev_slot[:], neg_ev[q][:].indirect(picks), ACT.Copy)
+                gap_slot = ring.tile([P, 256], F32, name="gap_slot")
+                if q == 3:
+                    nc.vector.tensor_copy(gap_slot[:], gap_unit[q][:].indirect(picks))
+                else:
+                    nc.scalar.activation(gap_slot[:], gap_unit[q][:].indirect(picks), ACT.Copy)
+                zg = ps_turn.tile([P, HALF], F32, name="turned")
+                for b in range(2):
+                    cols = slice(P * b, P * b + P)
+                    r0 = 256 * rh + P * b
+                    turn(zg[:, cols], thr_sb[:, q, r0 : r0 + P], True, False)
+                    turn(zg[:, cols], ev_slot[:, cols], False, True)
+                for b in range(2):
+                    turn(zg[:, 256 + P * b : 256 + P * b + P], gap_slot[:, P * b : P * b + P])
+                keepish = ring.tile([P, 256], F32, name="keepish")
+                nc.scalar.activation(keepish[:], zg[:, :256], ACT.Tanh, scale=-1.0)
+                nc.vector.scalar_tensor_tensor(
+                    hid_t[rh][:, :, P * q : P * q + P],
+                    keepish[:].rearrange("p (b f) -> p b f", b=2),
+                    1.0,
+                    zg[:, 256:].rearrange("p (b f) -> p b f", b=2),
+                    ALU.add,
+                    ALU.mult,
+                )
+
+        for rh in range(2):
+            pairs = ps_turn.tile([P, HALF], F32, name="turned")
+            for b in range(2):
+                words = hid_t[rh][:, b, :].bitcast(F32)
+                for u in range(2):
+                    c0 = 256 * b + P * u
+                    turn(pairs[:, c0 : c0 + P], words[:, u::2])
+            grouped = ring.tile([P, 256 * 4], BF16, name="grouped", align_bytes=64)
+            nc.vector.tensor_copy(
+                grouped[:].bitcast(F32).rearrange("p (b r u) -> p b r u", b=2, u=2),
+                pairs[:].rearrange("p (b u r) -> p b r u", b=2, u=2),
+            )
+            codes = ring.tile([P, 256], U32, name="codes", align_bytes=64)
+            planes = ring.tile([P, 256], U8, name="planes", align_bytes=64)
+            nc.vector.quantize_mx(codes[:].bitcast(FP8X4), planes[:], grouped[:])
+            acc = ps_turn.tile([P, HALF], F32, name="turned")
+            for mt in range(2):
+                nc.tensor.matmul_mx(
+                    acc[:, 256 * mt : 256 * mt + 256],
+                    lhsT=w2w[:, 256 * mt : 256 * mt + 256].bitcast(FP4X4),
+                    lhsT_scale=w2s[:, P * mt : P * mt + P],
+                    rhs=codes[:].bitcast(FP8X4),
+                    rhs_scale=planes[:],
+                    start=True,
+                    stop=True,
+                )
+            res = ring.tile([P, 2, 256], F32, name="res")
+            nc.scalar.copy(res[:], acc[:].rearrange("p (m r) -> p m r", m=2))
+            nc.sync.dma_start(
+                out.rearrange("(m p) r -> p m r", p=P)[:, :, 256 * rh : 256 * rh + 256], res[:]
+            )

@@ -23,6 +23,7 @@ PASSES = K // 512
 QUARTERS = H // P
 HALF = 512
 WINDOW = V + 16
+SK = 0.5
 GUESS_SLOPE, GUESS_SHIFT, GUESS_FLOOR = -0.9609375, 0.6875, 0.2135
 
 
@@ -32,34 +33,31 @@ def tile_picked_ymaskd_gap_p_kernel(
     nc = tc.nc
     with ExitStack() as ctx:
         keep = ctx.enter_context(tc.tile_pool(name="keep", bufs=1))
-        ring = ctx.enter_context(tc.tile_pool(name="ring", bufs=3))
-        ps_y = ctx.enter_context(tc.psum_pool(name="ps_y", bufs=3))
-        ps_sum = ctx.enter_context(tc.psum_pool(name="ps_sum", bufs=1))
-        ps_turn = ctx.enter_context(tc.psum_pool(name="ps_turn", bufs=3))
+        ring = ctx.enter_context(tc.tile_pool(name="ring", bufs=4))
+        wide = ctx.enter_context(tc.tile_pool(name="wide", bufs=8))
+        psum = ctx.enter_context(tc.psum_pool(name="psum", bufs=8))
 
         offs_sb = keep.tile([P, S // 16], U16, name="offs_sb")
         nc.sync.dma_start(offs_sb[:], offs)
 
         xs = keep.tile([P, T], U8, name="xs", align_bytes=64)
-        nc.vector.memset(xs[:].bitcast(I32), 0)
-        for quad in range(4):
-            nc.sync.dma_start(
-                xs[32 * quad : 32 * quad + 8, :].bitcast(I32),
-                x_scales[:, 4 * quad : 4 * quad + 4, :].bitcast(I32),
-            )
+        nc.sync.dma_start(xs[96:, :].bitcast(I32), x_scales.rearrange("o g c -> g o c").bitcast(I32))
+        nc.vector.memset(xs[:96, :].bitcast(I32), 0)
         xw = [keep.tile([P, T], U32, name="xw%d" % o, align_bytes=64) for o in range(PASSES)]
         w1w = keep.tile([P, PASSES, 2 * H], U8, name="w1w", align_bytes=64)
         nc.sync.dma_start(xw[0][:].bitcast(I32), x_words[0].rearrange("p n t -> p (n t)").bitcast(I32))
-        nc.sync.dma_start(w1w[:].bitcast(I32), w1_words.rearrange("o p c -> p o c").bitcast(I32))
         nc.sync.dma_start(xw[1][:].bitcast(I32), x_words[1].rearrange("p n t -> p (n t)").bitcast(I32))
+        nc.sync.dma_start(w1w[:].bitcast(I32), w1_words.rearrange("o p c -> p o c").bitcast(I32))
 
         w1s = keep.tile([P, PASSES, H], U8, name="w1s", align_bytes=64)
         nc.gpsimd.memset(w1s[:].bitcast(I32), 0)
         for quad in range(4):
-            nc.gpsimd.dma_start(
+            nc.scalar.dma_start(
                 w1s[32 * quad : 32 * quad + 4, :, :].bitcast(I32),
                 w1_scales[:, 4 * quad : 4 * quad + 4, :].rearrange("o r c -> r o c").bitcast(I32),
             )
+        gs = keep.tile([P, PASSES, S], U8, name="gs", align_bytes=64)
+        nc.gpsimd.memset(gs[:].bitcast(I32), 0)
 
         ident = keep.tile([P, P], F32, name="ident")
         make_identity(nc, ident[:])
@@ -67,44 +65,39 @@ def tile_picked_ymaskd_gap_p_kernel(
         nc.gpsimd.memset(consts[:, 0:1], GUESS_SHIFT)
         nc.gpsimd.memset(consts[:, 1:2], 1.0)
         nc.gpsimd.memset(consts[:, 2:3], 0.5)
-
-        slot_sb = keep.tile([P, U // 16], U16, name="slot_sb")
-        nc.sync.dma_start(slot_sb[:], slot)
-        thr_sb = keep.tile([P, QUARTERS, U], F32, name="thr_sb")
-        nc.sync.dma_start(thr_sb[:], thr.rearrange("(q p) r -> p q r", p=P))
-        w2w = keep.tile([P, 2 * N], U8, name="w2w", align_bytes=64)
-        nc.sync.dma_start(w2w[:].bitcast(I32), w2_words[0].bitcast(I32))
-
-        unit_sb = keep.tile([P, QUARTERS], F32, name="unit_sb")
-        with nc.allow_non_contiguous_dma(reason="one value a partition and quarter"):
-            nc.gpsimd.dma_start(unit_sb[:], unit.rearrange("(q p) o -> p (q o)", p=P))
-        half_unit = keep.tile([P, QUARTERS], F32, name="half_unit")
-        nc.gpsimd.tensor_scalar(half_unit[:], unit_sb[:], 0.5, 0.0, ALU.mult, ALU.add)
-
         w2s = keep.tile([P, N], U8, name="w2s", align_bytes=64)
         nc.gpsimd.memset(w2s[:].bitcast(I32), 0)
-        for quad in range(4):
-            nc.gpsimd.dma_start(
-                w2s[32 * quad : 32 * quad + 4, :].bitcast(I32),
-                w2_scales[0, 4 * quad : 4 * quad + 4, :].bitcast(I32),
-            )
-
         neg_ev = [keep.tile([P, WINDOW], F32, name="neg_ev%d" % q) for q in range(QUARTERS)]
         gap_unit = [keep.tile([P, WINDOW], F32, name="gap_unit%d" % q) for q in range(QUARTERS)]
         for q in range(QUARTERS):
             nc.gpsimd.memset(neg_ev[q][:, V:], 0.0)
             nc.gpsimd.memset(gap_unit[q][:, V:], 0.0)
 
-        gs0 = keep.tile([P, S], U8, name="gs0", align_bytes=64)
-        nc.vector.tensor_copy(gs0[:], xs[:].indirect(offs_sb[:]))
-        gs1 = keep.tile([P, S], U8, name="gs1", align_bytes=64)
-        nc.vector.memset(gs1[:].bitcast(I32), 0)
+        picked_rows = keep.tile([P, S], U8, name="picked_rows", align_bytes=64)
+        nc.vector.tensor_copy(picked_rows[:], xs[:].indirect(offs_sb[:]))
         for quad in range(4):
             nc.scalar.dma_start(
-                gs1[32 * quad : 32 * quad + 4, :].bitcast(I32),
-                gs0[32 * quad + 4 : 32 * quad + 8, :].bitcast(I32),
+                gs[32 * quad : 32 * quad + 4, :, :].bitcast(I32),
+                picked_rows[96 + 8 * quad : 96 + 8 * quad + 8, :].bitcast(I32),
             )
-        gs = [gs0, gs1]
+
+        slot_sb = keep.tile([P, U // 16], U16, name="slot_sb")
+        nc.sync.dma_start(slot_sb[:], slot)
+        unit_sb = keep.tile([P, QUARTERS], F32, name="unit_sb")
+        with nc.allow_non_contiguous_dma(reason="one value a partition and quarter"):
+            nc.sync.dma_start(unit_sb[:], unit.rearrange("(q p) o -> p (q o)", p=P))
+        half_unit = keep.tile([P, QUARTERS], F32, name="half_unit")
+        nc.gpsimd.tensor_scalar(half_unit[:], unit_sb[:], 0.5, 0.0, ALU.mult, ALU.add)
+        thr_sb = keep.tile([P, QUARTERS, U], F32, name="thr_sb")
+        nc.sync.dma_start(thr_sb[:], thr.rearrange("(q p) r -> p q r", p=P))
+        w2w = keep.tile([P, 2 * N], U8, name="w2w", align_bytes=64)
+        nc.sync.dma_start(w2w[:].bitcast(I32), w2_words[0].bitcast(I32))
+        for quad in range(4):
+            nc.sync.dma_start(
+                w2s[32 * quad : 32 * quad + 4, :].bitcast(I32),
+                w2_scales[0, 4 * quad : 4 * quad + 4, :].bitcast(I32),
+            )
+
         gw = {}
         for o in range(PASSES):
             for h in range(2):
@@ -116,118 +109,187 @@ def tile_picked_ymaskd_gap_p_kernel(
         def turn(dst, src, start=True, stop=True):
             nc.tensor.matmul(dst, src, ident[:], start=start, stop=stop, is_transpose=True)
 
-        for q in range(QUARTERS):
-            best = keep.tile([P, V], F32, name="best%d" % q)
-            sum_e = ps_sum.tile([P, V], F32, name="sum_e")
-            sum_p = ps_sum.tile([P, V], F32, name="sum_p")
-            for h in range(2):
-                y = ps_y.tile([P, HALF], F32, name="y")
+        scores = {}
+        for h in range(2):
+            for q in range(QUARTERS):
+                y = scores[q, h] = psum.tile([P, HALF], F32, name="bank")
                 for o in range(PASSES):
                     nc.tensor.matmul_mx(
                         y[:],
                         lhsT=w1w[:, o, 256 * q : 256 * q + 256].bitcast(FP4X4),
                         lhsT_scale=w1s[:, o, P * q : P * q + P],
                         rhs=gw[o, h][:].bitcast(FP8X4),
-                        rhs_scale=gs[o][:, HALF * h : HALF * h + HALF],
+                        rhs_scale=gs[:, o, HALF * h : HALF * h + HALF],
                         start=(o == 0),
                         stop=(o == PASSES - 1),
                     )
-                top = best[:, P * h : P * h + P]
-                nc.vector.tensor_reduce(top, y[:].rearrange("p (v d) -> p v d", d=D), AX.X, ALU.max)
-                diff = ring.tile([P, D, P], F32, name="diff")
-                nc.vector.tensor_tensor(
-                    diff[:],
-                    y[:].rearrange("p (v d) -> p d v", d=D),
-                    top.unsqueeze(1).to_broadcast([P, D, P]),
-                    ALU.subtract,
-                )
-                expd = ring.tile([P, D, P], F32, name="expd")
-                nc.scalar.activation(expd[:], diff[:], ACT.Exp)
-                for d in range(D):
-                    turn(sum_e[:, P * h : P * h + P], expd[:, d, :], d == 0, d == D - 1)
-                prod = ring.tile([P, D, P], F32, name="prod")
-                nc.vector.tensor_tensor(prod[:], expd[:], diff[:], ALU.mult)
-                for d in range(D):
-                    turn(sum_p[:, P * h : P * h + P], prod[:, d, :], d == 0, d == D - 1)
 
-            guess = ring.tile([P, V], F32, name="guess")
-            nc.scalar.activation(guess[:], sum_e[:], ACT.Exp, bias=consts[:, 0:1], scale=GUESS_SLOPE)
-            near_one = ring.tile([P, V], F32, name="near_one")
-            nc.vector.scalar_tensor_tensor(near_one[:], guess[:], GUESS_FLOOR, sum_e[:], ALU.add, ALU.mult)
-            err2 = ring.tile([P, V], F32, name="err2")
-            nc.scalar.activation(err2[:], near_one[:], ACT.Square, bias=consts[:, 1:2], scale=-1.0)
-            series = ring.tile([P, V], F32, name="series")
+        best = [keep.tile([P, V], F32, name="best%d" % q) for q in range(QUARTERS)]
+        t = {}
+
+        def largest(q, h):
+            nc.vector.tensor_reduce(
+                best[q][:, P * h : P * h + P], scores[q, h][:].rearrange("p (v d) -> p v d", d=D), AX.X, ALU.max
+            )
+
+        def shifted(q, h):
+            diff = t["diff", q, h] = wide.tile([P, D, P], F32, name="diff")
+            nc.vector.tensor_tensor(
+                diff[:],
+                scores[q, h][:].rearrange("p (v d) -> p d v", d=D),
+                best[q][:, P * h : P * h + P].unsqueeze(1).to_broadcast([P, D, P]),
+                ALU.subtract,
+            )
+
+        def weights(q, h):
+            expd = t["expd", q, h] = wide.tile([P, D, P], F32, name="expd")
+            nc.scalar.activation(expd[:], t["diff", q, h][:], ACT.Exp)
+
+        def weighted(q, h):
+            if h == 0:
+                t["sum_e", q] = psum.tile([P, V], F32, name="bank")
+            for d in range(D):
+                turn(t["sum_e", q][:, P * h : P * h + P], t["expd", q, h][:, d, :], d == 0, d == D - 1)
+            prod = t["prod", q, h] = wide.tile([P, D, P], F32, name="prod")
+            (nc.gpsimd).tensor_tensor(prod[:], t["expd", q, h][:], t["diff", q, h][:], ALU.mult)
+
+        def summed(q, h):
+            if h == 0:
+                t["sum_p", q] = psum.tile([P, V], F32, name="bank")
+            for d in range(D):
+                turn(t["sum_p", q][:, P * h : P * h + P], t["prod", q, h][:, d, :], d == 0, d == D - 1)
+
+        def g0(q):
+            guess = t["guess", q] = ring.tile([P, V], F32, name="guess")
+            nc.scalar.activation(guess[:], t["sum_e", q][:], ACT.Exp, bias=consts[:, 0:1], scale=GUESS_SLOPE)
+
+        def g1(q):
+            near_one = t["near", q] = ring.tile([P, V], F32, name="near_one")
+            nc.vector.scalar_tensor_tensor(near_one[:], t["guess", q][:], GUESS_FLOOR, t["sum_e", q][:], ALU.add, ALU.mult)
+
+        def g1b(q):
+            quot0 = t["q0", q] = ring.tile([P, V], F32, name="quot0")
+            nc.vector.scalar_tensor_tensor(quot0[:], t["guess", q][:], GUESS_FLOOR, t["sum_p", q][:], ALU.add, ALU.mult)
+
+        def g2(q):
+            err2 = t["err2", q] = ring.tile([P, V], F32, name="err2")
+            nc.scalar.activation(err2[:], t["near", q][:], ACT.Square, bias=consts[:, 1:2], scale=-1.0)
+
+        def g2b(q):
+            err2 = t["err2", q]
+            series = t["series", q] = ring.tile([P, V], F32, name="series")
             nc.scalar.activation(series[:], err2[:], ACT.Square, bias=consts[:, 2:3], scale=1.0)
-            quot0 = ring.tile([P, V], F32, name="quot0")
-            nc.vector.scalar_tensor_tensor(quot0[:], guess[:], GUESS_FLOOR, sum_p[:], ALU.add, ALU.mult)
-            quot1 = ring.tile([P, V], F32, name="quot1")
-            nc.vector.scalar_tensor_tensor(quot1[:], near_one[:], -2.0, quot0[:], ALU.add, ALU.mult)
-            gap_t = ring.tile([P, V], F32, name="gap_t")
-            nc.vector.scalar_tensor_tensor(gap_t[:], series[:], 0.75, quot1[:], ALU.add, ALU.mult)
 
-            gap = ps_turn.tile([P, HALF], F32, name="turned")
+        def g2c(q):
+            quot1 = t["q1", q] = ring.tile([P, V], F32, name="quot1")
+            nc.vector.scalar_tensor_tensor(quot1[:], t["near", q][:], -2.0, t["q0", q][:], ALU.add, ALU.mult)
+
+        def g3(q):
+            gap_t = t["gap_t", q] = ring.tile([P, V], F32, name="gap_t")
+            nc.vector.scalar_tensor_tensor(gap_t[:], t["series", q][:], 0.75, t["q1", q][:], ALU.add, ALU.mult)
+
+        def g4(q):
+            gap = t["gap", q] = psum.tile([P, HALF], F32, name="bank")
             for h in range(2):
-                turn(gap[:, P * h : P * h + P], gap_t[:, P * h : P * h + P])
-            nc.vector.tensor_tensor(neg_ev[q][:, :V], gap[:, :V], best[:], ALU.subtract)
+                turn(gap[:, P * h : P * h + P], t["gap_t", q][:, P * h : P * h + P])
+
+        def g5(q):
+            gap = t["gap", q]
+            nc.vector.tensor_tensor(neg_ev[q][:, :V], gap[:, :V], best[q][:], ALU.subtract)
+
+        def g5b(q):
+            gap = t["gap", q]
             nc.scalar.activation(gap_unit[q][:, :V], gap[:, :V], ACT.Copy, scale=half_unit[:, q : q + 1])
 
-        for q in range(QUARTERS):
-            for rh in range(2):
-                picks = slot_sb[:, 16 * rh : 16 * rh + 16]
-                ev_slot = ring.tile([P, 256], F32, name="ev_slot")
-                nc.scalar.activation(ev_slot[:], neg_ev[q][:].indirect(picks), ACT.Copy)
-                gap_slot = ring.tile([P, 256], F32, name="gap_slot")
-                if q == 3:
-                    nc.vector.tensor_copy(gap_slot[:], gap_unit[q][:].indirect(picks))
-                else:
-                    nc.scalar.activation(gap_slot[:], gap_unit[q][:].indirect(picks), ACT.Copy)
-                zg = ps_turn.tile([P, HALF], F32, name="turned")
-                for b in range(2):
-                    cols = slice(P * b, P * b + P)
-                    r0 = 256 * rh + P * b
-                    turn(zg[:, cols], thr_sb[:, q, r0 : r0 + P], True, False)
-                    turn(zg[:, cols], ev_slot[:, cols], False, True)
-                for b in range(2):
-                    turn(zg[:, 256 + P * b : 256 + P * b + P], gap_slot[:, P * b : P * b + P])
-                keepish = ring.tile([P, 256], F32, name="keepish")
-                nc.scalar.activation(keepish[:], zg[:, :256], ACT.Tanh, scale=-1.0)
-                nc.vector.scalar_tensor_tensor(
-                    hid_t[rh][:, :, P * q : P * q + P],
-                    keepish[:].rearrange("p (b f) -> p b f", b=2),
-                    1.0,
-                    zg[:, 256:].rearrange("p (b f) -> p b f", b=2),
-                    ALU.add,
-                    ALU.mult,
-                )
+        def k0(q, rh):
+            picks = slot_sb[:, 16 * rh : 16 * rh + 16]
+            ev_slot = t["ev_slot", q, rh] = wide.tile([P, 256], F32, name="ev_slot")
+            nc.scalar.activation(ev_slot[:], neg_ev[q][:].indirect(picks), ACT.Copy)
 
-        for rh in range(2):
-            pairs = ps_turn.tile([P, HALF], F32, name="turned")
+        def k0b(q, rh):
+            picks = slot_sb[:, 16 * rh : 16 * rh + 16]
+            gap_slot = t["gap_slot", q, rh] = wide.tile([P, 256], F32, name="gap_slot")
+            if q >= 0:
+                nc.vector.tensor_copy(gap_slot[:], gap_unit[q][:].indirect(picks))
+            else:
+                nc.scalar.activation(gap_slot[:], gap_unit[q][:].indirect(picks), ACT.Copy)
+
+        def k1(q, rh):
+            zg = t["zg", q, rh] = psum.tile([P, HALF], F32, name="bank")
+            for b in range(2):
+                cols = slice(P * b, P * b + P)
+                r0 = 256 * rh + P * b
+                turn(zg[:, cols], thr_sb[:, q, r0 : r0 + P], True, False)
+                turn(zg[:, cols], t["ev_slot", q, rh][:, cols], False, True)
+            for b in range(2):
+                turn(zg[:, 256 + P * b : 256 + P * b + P], t["gap_slot", q, rh][:, P * b : P * b + P])
+
+        def k2(q, rh):
+            keepish = t["keepish", q, rh] = wide.tile([P, 256], F32, name="keepish")
+            nc.scalar.activation(keepish[:], t["zg", q, rh][:, :256], ACT.Tanh, scale=-1.0)
+
+        def k3(q, rh):
+            nc.vector.scalar_tensor_tensor(
+                hid_t[rh][:, :, P * q : P * q + P],
+                t["keepish", q, rh][:].rearrange("p (b f) -> p b f", b=2),
+                1.0,
+                t["zg", q, rh][:, 256:].rearrange("p (b f) -> p b f", b=2),
+                ALU.add,
+                ALU.mult,
+            )
+
+        def e0(rh):
+            pairs = t["pairs", rh] = psum.tile([P, HALF], F32, name="bank")
             for b in range(2):
                 words = hid_t[rh][:, b, :].bitcast(F32)
                 for u in range(2):
                     c0 = 256 * b + P * u
                     turn(pairs[:, c0 : c0 + P], words[:, u::2])
-            grouped = ring.tile([P, 256 * 4], BF16, name="grouped", align_bytes=64)
-            nc.vector.tensor_copy(
+
+        def e1(rh):
+            grouped = t["grouped", rh] = ring.tile([P, 256 * 4], BF16, name="grouped", align_bytes=64)
+            nc.scalar.copy(
                 grouped[:].bitcast(F32).rearrange("p (b r u) -> p b r u", b=2, u=2),
-                pairs[:].rearrange("p (b u r) -> p b r u", b=2, u=2),
+                t["pairs", rh][:].rearrange("p (b u r) -> p b r u", b=2, u=2),
             )
-            codes = ring.tile([P, 256], U32, name="codes", align_bytes=64)
-            planes = ring.tile([P, 256], U8, name="planes", align_bytes=64)
-            nc.vector.quantize_mx(codes[:].bitcast(FP8X4), planes[:], grouped[:])
-            acc = ps_turn.tile([P, HALF], F32, name="turned")
+
+        def e2(rh):
+            codes = t["codes", rh] = ring.tile([P, 256], U32, name="codes", align_bytes=64)
+            planes = t["planes", rh] = ring.tile([P, 256], U8, name="planes", align_bytes=64)
+            nc.vector.quantize_mx(codes[:].bitcast(FP8X4), planes[:], t["grouped", rh][:])
+
+        def e3(rh):
+            acc = t["acc", rh] = psum.tile([P, HALF], F32, name="bank")
             for mt in range(2):
                 nc.tensor.matmul_mx(
                     acc[:, 256 * mt : 256 * mt + 256],
                     lhsT=w2w[:, 256 * mt : 256 * mt + 256].bitcast(FP4X4),
                     lhsT_scale=w2s[:, P * mt : P * mt + P],
-                    rhs=codes[:].bitcast(FP8X4),
-                    rhs_scale=planes[:],
+                    rhs=t["codes", rh][:].bitcast(FP8X4),
+                    rhs_scale=t["planes", rh][:],
                     start=True,
                     stop=True,
                 )
+
+        def e4(rh):
             res = ring.tile([P, 2, 256], F32, name="res")
-            nc.scalar.copy(res[:], acc[:].rearrange("p (m r) -> p m r", m=2))
+            nc.scalar.copy(res[:], t["acc", rh][:].rearrange("p (m r) -> p m r", m=2))
             nc.sync.dma_start(
                 out.rearrange("(m p) r -> p m r", p=P)[:, :, 256 * rh : 256 * rh + 256], res[:]
             )
+
+        plan = []
+        for q in range(QUARTERS):
+            for h in range(2):
+                for k, step in enumerate((largest, shifted, weights, weighted, summed)):
+                    plan.append((SK * (2 * q + h) + 1 + k, len(plan), step, (q, h)))
+            for k, step in ((0, g0), (1, g1), (2, g2), (3, g2b), (2, g1b), (3, g2c), (4, g3), (5, g4), (6, g5), (7, g5b)):
+                plan.append((SK * (2 * q + 1) + 5 + k + (0.01 if k == 0 else 0), len(plan), step, (q,)))
+            for rh in range(2):
+                for k, step in enumerate((k0, k0b, k1, k2, k3)):
+                    plan.append((SK * (2 * q + 1 + 0.5 * rh) + 12.01 + k, len(plan), step, (q, rh)))
+        for rh in range(2):
+            for k, step in enumerate((e0, e1, e2, e3, e4)):
+                plan.append((SK * (7 + 0.5 * rh) + 17.02 + k, len(plan), step, (rh,)))
+        for when, tie, step, args in sorted(plan, key=lambda e: e[:2]):
+            step(*args)

@@ -23,7 +23,7 @@ PASSES = K // 512
 QUARTERS = H // P
 HALF = 512
 WINDOW = V + 16
-SK = 0.5
+SK = 0.7
 GUESS_SLOPE, GUESS_SHIFT, GUESS_FLOOR = -0.9609375, 0.6875, 0.2135
 
 
@@ -52,12 +52,12 @@ def tile_picked_ymaskd_gap_p_kernel(
         w1s = keep.tile([P, PASSES, H], U8, name="w1s", align_bytes=64)
         nc.gpsimd.memset(w1s[:].bitcast(I32), 0)
         for quad in range(4):
-            nc.scalar.dma_start(
+            nc.gpsimd.dma_start(
                 w1s[32 * quad : 32 * quad + 4, :, :].bitcast(I32),
                 w1_scales[:, 4 * quad : 4 * quad + 4, :].rearrange("o r c -> r o c").bitcast(I32),
             )
         gs = keep.tile([P, PASSES, S], U8, name="gs", align_bytes=64)
-        nc.gpsimd.memset(gs[:].bitcast(I32), 0)
+        nc.vector.memset(gs[:].bitcast(I32), 0)
 
         ident = keep.tile([P, P], F32, name="ident")
         make_identity(nc, ident[:])
@@ -65,8 +65,6 @@ def tile_picked_ymaskd_gap_p_kernel(
         nc.gpsimd.memset(consts[:, 0:1], GUESS_SHIFT)
         nc.gpsimd.memset(consts[:, 1:2], 1.0)
         nc.gpsimd.memset(consts[:, 2:3], 0.5)
-        w2s = keep.tile([P, N], U8, name="w2s", align_bytes=64)
-        nc.gpsimd.memset(w2s[:].bitcast(I32), 0)
         neg_ev = [keep.tile([P, WINDOW], F32, name="neg_ev%d" % q) for q in range(QUARTERS)]
         gap_unit = [keep.tile([P, WINDOW], F32, name="gap_unit%d" % q) for q in range(QUARTERS)]
         for q in range(QUARTERS):
@@ -85,24 +83,27 @@ def tile_picked_ymaskd_gap_p_kernel(
         nc.sync.dma_start(slot_sb[:], slot)
         unit_sb = keep.tile([P, QUARTERS], F32, name="unit_sb")
         with nc.allow_non_contiguous_dma(reason="one value a partition and quarter"):
-            nc.sync.dma_start(unit_sb[:], unit.rearrange("(q p) o -> p (q o)", p=P))
+            nc.gpsimd.dma_start(unit_sb[:], unit.rearrange("(q p) o -> p (q o)", p=P))
         half_unit = keep.tile([P, QUARTERS], F32, name="half_unit")
         nc.gpsimd.tensor_scalar(half_unit[:], unit_sb[:], 0.5, 0.0, ALU.mult, ALU.add)
-        thr_sb = keep.tile([P, QUARTERS, U], F32, name="thr_sb")
-        nc.sync.dma_start(thr_sb[:], thr.rearrange("(q p) r -> p q r", p=P))
-        w2w = keep.tile([P, 2 * N], U8, name="w2w", align_bytes=64)
-        nc.sync.dma_start(w2w[:].bitcast(I32), w2_words[0].bitcast(I32))
-        for quad in range(4):
-            nc.sync.dma_start(
-                w2s[32 * quad : 32 * quad + 4, :].bitcast(I32),
-                w2_scales[0, 4 * quad : 4 * quad + 4, :].bitcast(I32),
-            )
 
         gw = {}
         for o in range(PASSES):
             for h in range(2):
                 gw[o, h] = keep.tile([P, HALF], U32, name="gw%d%d" % (o, h), align_bytes=64)
                 nc.vector.tensor_copy(gw[o, h][:], xw[o][:].indirect(offs_sb[:, 32 * h : 32 * h + 32]))
+
+        thr_sb = keep.tile([P, QUARTERS, U], F32, name="thr_sb", tag="xw0", align_bytes=64)
+        nc.sync.dma_start(thr_sb[:], thr.rearrange("(q p) r -> p q r", p=P))
+        w2s = keep.tile([P, N], U8, name="w2s", tag="xs", align_bytes=64)
+        nc.gpsimd.memset(w2s[:].bitcast(I32), 0)
+        w2w = keep.tile([P, 2 * N], U8, name="w2w", tag="xw1", align_bytes=64)
+        nc.sync.dma_start(w2w[:].bitcast(I32), w2_words[0].bitcast(I32))
+        for quad in range(4):
+            nc.sync.dma_start(
+                w2s[32 * quad : 32 * quad + 4, :].bitcast(I32),
+                w2_scales[0, 4 * quad : 4 * quad + 4, :].bitcast(I32),
+            )
 
         hid_t = [keep.tile([P, 2, H], BF16, name="hid_t%d" % rh, align_bytes=64) for rh in range(2)]
 
@@ -151,7 +152,7 @@ def tile_picked_ymaskd_gap_p_kernel(
             for d in range(D):
                 turn(t["sum_e", q][:, P * h : P * h + P], t["expd", q, h][:, d, :], d == 0, d == D - 1)
             prod = t["prod", q, h] = wide.tile([P, D, P], F32, name="prod")
-            (nc.gpsimd).tensor_tensor(prod[:], t["expd", q, h][:], t["diff", q, h][:], ALU.mult)
+            (nc.gpsimd if q < 3 else nc.vector).tensor_tensor(prod[:], t["expd", q, h][:], t["diff", q, h][:], ALU.mult)
 
         def summed(q, h):
             if h == 0:
@@ -238,45 +239,41 @@ def tile_picked_ymaskd_gap_p_kernel(
                 ALU.mult,
             )
 
-        def e0(rh):
-            pairs = t["pairs", rh] = psum.tile([P, HALF], F32, name="bank")
-            for b in range(2):
-                words = hid_t[rh][:, b, :].bitcast(F32)
-                for u in range(2):
-                    c0 = 256 * b + P * u
-                    turn(pairs[:, c0 : c0 + P], words[:, u::2])
+        def e0(rb):
+            pairs = t["pairs", rb] = psum.tile([P, 2, P], F32, name="bank")
+            words = hid_t[rb // 2][:, rb % 2, :].bitcast(F32)
+            for u in range(2):
+                turn(pairs[:, u, :], words[:, u::2])
 
-        def e1(rh):
-            grouped = t["grouped", rh] = ring.tile([P, 256 * 4], BF16, name="grouped", align_bytes=64)
-            nc.scalar.copy(
-                grouped[:].bitcast(F32).rearrange("p (b r u) -> p b r u", b=2, u=2),
-                t["pairs", rh][:].rearrange("p (b u r) -> p b r u", b=2, u=2),
+        def e1(rb):
+            grouped = t["grouped", rb] = ring.tile([P, P * 4], BF16, name="grouped", align_bytes=64)
+            (nc.vector.tensor_copy if rb % 2 else nc.scalar.copy)(
+                grouped[:].bitcast(F32).rearrange("p (r u) -> p r u", u=2),
+                t["pairs", rb][:].rearrange("p u r -> p r u"),
             )
 
-        def e2(rh):
-            codes = t["codes", rh] = ring.tile([P, 256], U32, name="codes", align_bytes=64)
-            planes = t["planes", rh] = ring.tile([P, 256], U8, name="planes", align_bytes=64)
-            nc.vector.quantize_mx(codes[:].bitcast(FP8X4), planes[:], t["grouped", rh][:])
+        def e2(rb):
+            codes = t["codes", rb] = ring.tile([P, P], U32, name="codes", align_bytes=64)
+            planes = t["planes", rb] = ring.tile([P, P], U8, name="planes", align_bytes=64)
+            nc.vector.quantize_mx(codes[:].bitcast(FP8X4), planes[:], t["grouped", rb][:])
 
-        def e3(rh):
-            acc = t["acc", rh] = psum.tile([P, HALF], F32, name="bank")
+        def e3(rb):
+            acc = t["acc", rb] = psum.tile([P, 2, P], F32, name="bank")
             for mt in range(2):
                 nc.tensor.matmul_mx(
-                    acc[:, 256 * mt : 256 * mt + 256],
+                    acc[:, mt, :],
                     lhsT=w2w[:, 256 * mt : 256 * mt + 256].bitcast(FP4X4),
                     lhsT_scale=w2s[:, P * mt : P * mt + P],
-                    rhs=t["codes", rh][:].bitcast(FP8X4),
-                    rhs_scale=t["planes", rh][:],
+                    rhs=t["codes", rb][:].bitcast(FP8X4),
+                    rhs_scale=t["planes", rb][:],
                     start=True,
                     stop=True,
                 )
 
-        def e4(rh):
-            res = ring.tile([P, 2, 256], F32, name="res")
-            nc.scalar.copy(res[:], t["acc", rh][:].rearrange("p (m r) -> p m r", m=2))
-            nc.sync.dma_start(
-                out.rearrange("(m p) r -> p m r", p=P)[:, :, 256 * rh : 256 * rh + 256], res[:]
-            )
+        def e4(rb):
+            res = ring.tile([P, 2, P], F32, name="res")
+            (nc.scalar.copy)(res[:], t["acc", rb][:])
+            nc.sync.dma_start(out.rearrange("(m p) r -> p m r", p=P)[:, :, P * rb : P * rb + P], res[:])
 
         plan = []
         for q in range(QUARTERS):
@@ -288,8 +285,8 @@ def tile_picked_ymaskd_gap_p_kernel(
             for rh in range(2):
                 for k, step in enumerate((k0, k0b, k1, k2, k3)):
                     plan.append((SK * (2 * q + 1 + 0.5 * rh) + 12.01 + k, len(plan), step, (q, rh)))
-        for rh in range(2):
+        for rb in range(4):
             for k, step in enumerate((e0, e1, e2, e3, e4)):
-                plan.append((SK * (7 + 0.5 * rh) + 17.02 + k, len(plan), step, (rh,)))
+                plan.append((SK * 7.5 + 0.1 * rb + 17.02 + k, len(plan), step, (rb,)))
         for when, tie, step, args in sorted(plan, key=lambda e: e[:2]):
             step(*args)

@@ -22,7 +22,7 @@ P = 128
 PASSES = K // 512
 QUARTERS = H // P
 HALF = 512
-WINDOW = V + 16
+WINDOW = 2 * V
 SK = 0.7
 GUESS_SLOPE, GUESS_SHIFT, GUESS_FLOOR = -0.9609375, 0.6875, 0.2135
 
@@ -62,14 +62,11 @@ def tile_picked_ymaskd_gap_p_kernel(
         ident = keep.tile([P, P], F32, name="ident")
         make_identity(nc, ident[:])
         consts = keep.tile([P, 3], F32, name="consts")
-        nc.gpsimd.memset(consts[:, 0:1], GUESS_SHIFT)
-        nc.gpsimd.memset(consts[:, 1:2], 1.0)
-        nc.gpsimd.memset(consts[:, 2:3], 0.5)
+        nc.vector.memset(consts[:, 0:1], GUESS_SHIFT)
+        nc.vector.memset(consts[:, 1:2], 1.0)
+        nc.vector.memset(consts[:, 2:3], 0.5)
         neg_ev = [keep.tile([P, WINDOW], F32, name="neg_ev%d" % q) for q in range(QUARTERS)]
         gap_unit = [keep.tile([P, WINDOW], F32, name="gap_unit%d" % q) for q in range(QUARTERS)]
-        for q in range(QUARTERS):
-            nc.gpsimd.memset(neg_ev[q][:, V:], 0.0)
-            nc.gpsimd.memset(gap_unit[q][:, V:], 0.0)
 
         picked_rows = keep.tile([P, S], U8, name="picked_rows", align_bytes=64)
         nc.vector.tensor_copy(picked_rows[:], xs[:].indirect(offs_sb[:]))
@@ -83,9 +80,9 @@ def tile_picked_ymaskd_gap_p_kernel(
         nc.sync.dma_start(slot_sb[:], slot)
         unit_sb = keep.tile([P, QUARTERS], F32, name="unit_sb")
         with nc.allow_non_contiguous_dma(reason="one value a partition and quarter"):
-            nc.gpsimd.dma_start(unit_sb[:], unit.rearrange("(q p) o -> p (q o)", p=P))
+            nc.scalar.dma_start(unit_sb[:], unit.rearrange("(q p) o -> p (q o)", p=P))
         half_unit = keep.tile([P, QUARTERS], F32, name="half_unit")
-        nc.gpsimd.tensor_scalar(half_unit[:], unit_sb[:], 0.5, 0.0, ALU.mult, ALU.add)
+        nc.scalar.activation(half_unit[:], unit_sb[:], ACT.Copy, scale=0.5)
 
         gw = {}
         for o in range(PASSES):
@@ -125,7 +122,7 @@ def tile_picked_ymaskd_gap_p_kernel(
                         stop=(o == PASSES - 1),
                     )
 
-        best = [keep.tile([P, V], F32, name="best%d" % q) for q in range(QUARTERS)]
+        best = [neg_ev[q][:, V:] for q in range(QUARTERS)]
         t = {}
 
         def largest(q, h):
@@ -186,8 +183,8 @@ def tile_picked_ymaskd_gap_p_kernel(
             nc.vector.scalar_tensor_tensor(quot1[:], t["near", q][:], -2.0, t["q0", q][:], ALU.add, ALU.mult)
 
         def g3(q):
-            gap_t = t["gap_t", q] = ring.tile([P, V], F32, name="gap_t")
-            nc.vector.scalar_tensor_tensor(gap_t[:], t["series", q][:], 0.75, t["q1", q][:], ALU.add, ALU.mult)
+            gap_t = t["gap_t", q] = gap_unit[q][:, V:]
+            nc.vector.scalar_tensor_tensor(gap_t, t["series", q][:], 0.75, t["q1", q][:], ALU.add, ALU.mult)
 
         def g4(q):
             gap = t["gap", q] = psum.tile([P, HALF], F32, name="bank")
@@ -196,7 +193,7 @@ def tile_picked_ymaskd_gap_p_kernel(
 
         def g5(q):
             gap = t["gap", q]
-            nc.vector.tensor_tensor(neg_ev[q][:, :V], gap[:, :V], best[q][:], ALU.subtract)
+            nc.vector.tensor_tensor(neg_ev[q][:, :V], gap[:, :V], best[q], ALU.subtract)
 
         def g5b(q):
             gap = t["gap", q]

@@ -20,11 +20,18 @@ AX = mybir.AxisListType
 
 P = 128
 PASSES = K // 512
+QUADS = 4
 QUARTERS = H // P
-HALF = 512
-WINDOW = 2 * V
-SK = 0.7
+LIST_HALF = S // 2
+SLOT_HALF = U // 2
+SLOT_BLOCKS = U // P
+ROWS_AT = 96
+
 GUESS_SLOPE, GUESS_SHIFT, GUESS_FLOOR = -0.9609375, 0.6875, 0.2135
+
+GPSIMD_QUARTERS = 3
+
+STEP, LAG = 20, 14
 
 
 def tile_picked_ymaskd_gap_p_kernel(
@@ -33,257 +40,252 @@ def tile_picked_ymaskd_gap_p_kernel(
     nc = tc.nc
     with ExitStack() as ctx:
         keep = ctx.enter_context(tc.tile_pool(name="keep", bufs=1))
-        ring = ctx.enter_context(tc.tile_pool(name="ring", bufs=4))
-        wide = ctx.enter_context(tc.tile_pool(name="wide", bufs=8))
+        per_quarter = ctx.enter_context(tc.tile_pool(name="per_quarter", bufs=QUARTERS))
+        per_half = ctx.enter_context(tc.tile_pool(name="per_half", bufs=2 * QUARTERS))
         psum = ctx.enter_context(tc.psum_pool(name="psum", bufs=8))
 
         offs_sb = keep.tile([P, S // 16], U16, name="offs_sb")
         nc.sync.dma_start(offs_sb[:], offs)
 
-        xs = keep.tile([P, T], U8, name="xs", align_bytes=64)
-        nc.sync.dma_start(xs[96:, :].bitcast(I32), x_scales.rearrange("o g c -> g o c").bitcast(I32))
-        nc.vector.memset(xs[:96, :].bitcast(I32), 0)
-        xw = [keep.tile([P, T], U32, name="xw%d" % o, align_bytes=64) for o in range(PASSES)]
-        w1w = keep.tile([P, PASSES, 2 * H], U8, name="w1w", align_bytes=64)
-        nc.sync.dma_start(xw[0][:].bitcast(I32), x_words[0].rearrange("p n t -> p (n t)").bitcast(I32))
-        nc.sync.dma_start(xw[1][:].bitcast(I32), x_words[1].rearrange("p n t -> p (n t)").bitcast(I32))
-        nc.sync.dma_start(w1w[:].bitcast(I32), w1_words.rearrange("o p c -> p o c").bitcast(I32))
+        x_rows = keep.tile([P, T], U8, name="x_rows", align_bytes=64)
+        nc.sync.dma_start(x_rows[ROWS_AT:, :].bitcast(I32), x_scales.rearrange("o g c -> g o c").bitcast(I32))
+        nc.vector.memset(x_rows[:ROWS_AT, :].bitcast(I32), 0)
+        x_table = [keep.tile([P, T], U32, name="x_table%d" % o, align_bytes=64) for o in range(PASSES)]
+        w1_codes = keep.tile([P, PASSES, 2 * H], U8, name="w1_codes", align_bytes=64)
+        for o in range(PASSES):
+            nc.sync.dma_start(x_table[o][:].bitcast(I32), x_words[o].rearrange("p n j -> p (n j)").bitcast(I32))
+        nc.sync.dma_start(w1_codes[:].bitcast(I32), w1_words.rearrange("o p c -> p o c").bitcast(I32))
 
-        w1s = keep.tile([P, PASSES, H], U8, name="w1s", align_bytes=64)
-        nc.gpsimd.memset(w1s[:].bitcast(I32), 0)
-        for quad in range(4):
+        w1_scale = keep.tile([P, PASSES, H], U8, name="w1_scale", align_bytes=64)
+        nc.gpsimd.memset(w1_scale[:].bitcast(I32), 0)
+        for quad in range(QUADS):
             nc.gpsimd.dma_start(
-                w1s[32 * quad : 32 * quad + 4, :, :].bitcast(I32),
+                w1_scale[32 * quad : 32 * quad + 4, :, :].bitcast(I32),
                 w1_scales[:, 4 * quad : 4 * quad + 4, :].rearrange("o r c -> r o c").bitcast(I32),
             )
-        gs = keep.tile([P, PASSES, S], U8, name="gs", align_bytes=64)
-        nc.vector.memset(gs[:].bitcast(I32), 0)
+        x_scale = [keep.tile([P, PASSES, LIST_HALF], U8, name="x_scale%d" % h, align_bytes=64) for h in range(2)]
+        for h in range(2):
+            nc.vector.memset(x_scale[h][:].bitcast(I32), 0)
 
         ident = keep.tile([P, P], F32, name="ident")
         make_identity(nc, ident[:])
-        consts = keep.tile([P, 3], F32, name="consts")
-        nc.vector.memset(consts[:, 0:1], GUESS_SHIFT)
-        nc.vector.memset(consts[:, 1:2], 1.0)
-        nc.vector.memset(consts[:, 2:3], 0.5)
-        neg_ev = [keep.tile([P, WINDOW], F32, name="neg_ev%d" % q) for q in range(QUARTERS)]
-        gap_unit = [keep.tile([P, WINDOW], F32, name="gap_unit%d" % q) for q in range(QUARTERS)]
+        biases = keep.tile([P, 3], F32, name="biases")
+        for column, value in enumerate((GUESS_SHIFT, 1.0, 0.5)):
+            nc.vector.memset(biases[:, column : column + 1], value)
+        bias_shift, bias_one, bias_half = biases[:, 0:1], biases[:, 1:2], biases[:, 2:3]
 
-        picked_rows = keep.tile([P, S], U8, name="picked_rows", align_bytes=64)
-        nc.vector.tensor_copy(picked_rows[:], xs[:].indirect(offs_sb[:]))
-        for quad in range(4):
-            nc.scalar.dma_start(
-                gs[32 * quad : 32 * quad + 4, :, :].bitcast(I32),
-                picked_rows[96 + 8 * quad : 96 + 8 * quad + 8, :].bitcast(I32),
-            )
+        ev_window = [keep.tile([P, 2 * V], F32, name="ev_window%d" % q) for q in range(QUARTERS)]
+        gap_window = [keep.tile([P, 2 * V], F32, name="gap_window%d" % q) for q in range(QUARTERS)]
+        best = [ev_window[q][:, V:] for q in range(QUARTERS)]
+        gap_turned = [gap_window[q][:, V:] for q in range(QUARTERS)]
+
+        for h in range(2):
+            picked_rows = keep.tile([P, LIST_HALF], U8, name="picked_rows%d" % h, align_bytes=64)
+            nc.vector.tensor_copy(picked_rows[:], x_rows[:].indirect(offs_sb[:, 32 * h : 32 * h + 32]))
+            for quad in range(QUADS):
+                first = ROWS_AT + 8 * quad
+                nc.scalar.dma_start(
+                    x_scale[h][32 * quad : 32 * quad + 4, :, :].bitcast(I32),
+                    picked_rows[first : first + 8, :].bitcast(I32),
+                )
 
         slot_sb = keep.tile([P, U // 16], U16, name="slot_sb")
         nc.sync.dma_start(slot_sb[:], slot)
-        unit_sb = keep.tile([P, QUARTERS], F32, name="unit_sb")
-        with nc.allow_non_contiguous_dma(reason="one value a partition and quarter"):
-            nc.scalar.dma_start(unit_sb[:], unit.rearrange("(q p) o -> p (q o)", p=P))
-        half_unit = keep.tile([P, QUARTERS], F32, name="half_unit")
-        nc.scalar.activation(half_unit[:], unit_sb[:], ACT.Copy, scale=0.5)
 
-        gw = {}
+        x_codes = {}
         for o in range(PASSES):
             for h in range(2):
-                gw[o, h] = keep.tile([P, HALF], U32, name="gw%d%d" % (o, h), align_bytes=64)
-                nc.vector.tensor_copy(gw[o, h][:], xw[o][:].indirect(offs_sb[:, 32 * h : 32 * h + 32]))
+                x_codes[o, h] = keep.tile([P, LIST_HALF], U32, name="x_codes%d%d" % (o, h), align_bytes=64)
+                nc.vector.tensor_copy(x_codes[o, h][:], x_table[o][:].indirect(offs_sb[:, 32 * h : 32 * h + 32]))
 
-        thr_sb = keep.tile([P, QUARTERS, U], F32, name="thr_sb", tag="xw0", align_bytes=64)
-        nc.sync.dma_start(thr_sb[:], thr.rearrange("(q p) r -> p q r", p=P))
-        w2s = keep.tile([P, N], U8, name="w2s", tag="xs", align_bytes=64)
-        nc.gpsimd.memset(w2s[:].bitcast(I32), 0)
-        w2w = keep.tile([P, 2 * N], U8, name="w2w", tag="xw1", align_bytes=64)
-        nc.sync.dma_start(w2w[:].bitcast(I32), w2_words[0].bitcast(I32))
-        for quad in range(4):
-            nc.sync.dma_start(
-                w2s[32 * quad : 32 * quad + 4, :].bitcast(I32),
-                w2_scales[0, 4 * quad : 4 * quad + 4, :].bitcast(I32),
-            )
-
-        hid_t = [keep.tile([P, 2, H], BF16, name="hid_t%d" % rh, align_bytes=64) for rh in range(2)]
+        hid_turned = [keep.tile([P, 2, H], BF16, name="hid_turned%d" % s, align_bytes=64) for s in range(2)]
 
         def turn(dst, src, start=True, stop=True):
             nc.tensor.matmul(dst, src, ident[:], start=start, stop=stop, is_transpose=True)
 
-        scores = {}
+        y = {}
         for h in range(2):
             for q in range(QUARTERS):
-                y = scores[q, h] = psum.tile([P, HALF], F32, name="bank")
+                y[q, h] = psum.tile([P, LIST_HALF], F32, name="bank")
                 for o in range(PASSES):
                     nc.tensor.matmul_mx(
-                        y[:],
-                        lhsT=w1w[:, o, 256 * q : 256 * q + 256].bitcast(FP4X4),
-                        lhsT_scale=w1s[:, o, P * q : P * q + P],
-                        rhs=gw[o, h][:].bitcast(FP8X4),
-                        rhs_scale=gs[:, o, HALF * h : HALF * h + HALF],
+                        y[q, h][:],
+                        lhsT=w1_codes[:, o, 2 * P * q : 2 * P * (q + 1)].bitcast(FP4X4),
+                        lhsT_scale=w1_scale[:, o, P * q : P * (q + 1)],
+                        rhs=x_codes[o, h][:].bitcast(FP8X4),
+                        rhs_scale=x_scale[h][:, o, :],
                         start=(o == 0),
                         stop=(o == PASSES - 1),
                     )
 
-        best = [neg_ev[q][:, V:] for q in range(QUARTERS)]
-        t = {}
+        thr_sb = keep.tile([P, QUARTERS, U], F32, name="thr_sb", tag="x_table1", align_bytes=64)
+        nc.sync.dma_start(thr_sb[:], thr.rearrange("(q p) r -> p q r", p=P))
+        w2_scale = keep.tile([P, N], U8, name="w2_scale", tag="x_codes00", align_bytes=64)
+        nc.gpsimd.memset(w2_scale[:].bitcast(I32), 0)
+        w2_codes = keep.tile([P, 2 * N], U8, name="w2_codes", tag="x_table0", align_bytes=64)
+        nc.sync.dma_start(w2_codes[:].bitcast(I32), w2_words[0].bitcast(I32))
+        for quad in range(QUADS):
+            nc.sync.dma_start(
+                w2_scale[32 * quad : 32 * quad + 4, :].bitcast(I32),
+                w2_scales[0, 4 * quad : 4 * quad + 4, :].bitcast(I32),
+            )
+        unit_sb = keep.tile([P, QUARTERS], F32, name="unit_sb", tag="x_codes10", align_bytes=64)
+        with nc.allow_non_contiguous_dma(reason="one value for each partition and quarter"):
+            nc.sync.dma_start(unit_sb[:], unit.rearrange("(q p) o -> p (q o)", p=P))
+        half_unit = keep.tile([P, QUARTERS], F32, name="half_unit")
+        nc.scalar.activation(half_unit[:], unit_sb[:], ACT.Copy, scale=0.5)
+
+        diff, e, prod, sum_e, sum_p = {}, {}, {}, {}, {}
+        guess, near_one, err2, series, quot0, quot1, gap = {}, {}, {}, {}, {}, {}, {}
+        neg_ev_slot, gap_slot, turned, tanh_z = {}, {}, {}, {}
+        pairs, grouped, hid_codes, hid_scale, acc = {}, {}, {}, {}, {}
 
         def largest(q, h):
-            nc.vector.tensor_reduce(
-                best[q][:, P * h : P * h + P], scores[q, h][:].rearrange("p (v d) -> p v d", d=D), AX.X, ALU.max
-            )
+            members = y[q, h][:].rearrange("p (v d) -> p v d", d=D)
+            nc.vector.tensor_reduce(best[q][:, P * h : P * (h + 1)], members, AX.X, ALU.max)
 
-        def shifted(q, h):
-            diff = t["diff", q, h] = wide.tile([P, D, P], F32, name="diff")
-            nc.vector.tensor_tensor(
-                diff[:],
-                scores[q, h][:].rearrange("p (v d) -> p d v", d=D),
-                best[q][:, P * h : P * h + P].unsqueeze(1).to_broadcast([P, D, P]),
-                ALU.subtract,
-            )
+        def subtract_largest(q, h):
+            diff[q, h] = per_half.tile([P, D, P], F32, name="diff")
+            top = best[q][:, P * h : P * (h + 1)].unsqueeze(1).to_broadcast([P, D, P])
+            nc.vector.tensor_tensor(diff[q, h][:], y[q, h][:].rearrange("p (v d) -> p d v", d=D), top, ALU.subtract)
 
-        def weights(q, h):
-            expd = t["expd", q, h] = wide.tile([P, D, P], F32, name="expd")
-            nc.scalar.activation(expd[:], t["diff", q, h][:], ACT.Exp)
+        def exponentiate(q, h):
+            e[q, h] = per_half.tile([P, D, P], F32, name="e")
+            nc.scalar.activation(e[q, h][:], diff[q, h][:], ACT.Exp)
 
-        def weighted(q, h):
+        def sum_e_and_multiply(q, h):
             if h == 0:
-                t["sum_e", q] = psum.tile([P, V], F32, name="bank")
+                sum_e[q] = psum.tile([P, V], F32, name="bank")
             for d in range(D):
-                turn(t["sum_e", q][:, P * h : P * h + P], t["expd", q, h][:, d, :], d == 0, d == D - 1)
-            prod = t["prod", q, h] = wide.tile([P, D, P], F32, name="prod")
-            (nc.gpsimd if q < 3 else nc.vector).tensor_tensor(prod[:], t["expd", q, h][:], t["diff", q, h][:], ALU.mult)
+                turn(sum_e[q][:, P * h : P * (h + 1)], e[q, h][:, d, :], d == 0, d == D - 1)
+            prod[q, h] = per_half.tile([P, D, P], F32, name="prod")
+            engine = nc.gpsimd if q < GPSIMD_QUARTERS else nc.vector
+            engine.tensor_tensor(prod[q, h][:], e[q, h][:], diff[q, h][:], ALU.mult)
 
-        def summed(q, h):
+        def sum_products(q, h):
             if h == 0:
-                t["sum_p", q] = psum.tile([P, V], F32, name="bank")
+                sum_p[q] = psum.tile([P, V], F32, name="bank")
             for d in range(D):
-                turn(t["sum_p", q][:, P * h : P * h + P], t["prod", q, h][:, d, :], d == 0, d == D - 1)
+                turn(sum_p[q][:, P * h : P * (h + 1)], prod[q, h][:, d, :], d == 0, d == D - 1)
 
-        def g0(q):
-            guess = t["guess", q] = ring.tile([P, V], F32, name="guess")
-            nc.scalar.activation(guess[:], t["sum_e", q][:], ACT.Exp, bias=consts[:, 0:1], scale=GUESS_SLOPE)
+        def make_guess(q):
+            guess[q] = per_quarter.tile([P, V], F32, name="guess")
+            nc.scalar.activation(guess[q][:], sum_e[q][:], ACT.Exp, bias=bias_shift, scale=GUESS_SLOPE)
 
-        def g1(q):
-            near_one = t["near", q] = ring.tile([P, V], F32, name="near_one")
-            nc.vector.scalar_tensor_tensor(near_one[:], t["guess", q][:], GUESS_FLOOR, t["sum_e", q][:], ALU.add, ALU.mult)
+        def make_near_one(q):
+            near_one[q] = per_quarter.tile([P, V], F32, name="near_one")
+            nc.vector.scalar_tensor_tensor(near_one[q][:], guess[q][:], GUESS_FLOOR, sum_e[q][:], ALU.add, ALU.mult)
 
-        def g1b(q):
-            quot0 = t["q0", q] = ring.tile([P, V], F32, name="quot0")
-            nc.vector.scalar_tensor_tensor(quot0[:], t["guess", q][:], GUESS_FLOOR, t["sum_p", q][:], ALU.add, ALU.mult)
+        def make_err2(q):
+            err2[q] = per_quarter.tile([P, V], F32, name="err2")
+            nc.scalar.activation(err2[q][:], near_one[q][:], ACT.Square, bias=bias_one, scale=-1.0)
 
-        def g2(q):
-            err2 = t["err2", q] = ring.tile([P, V], F32, name="err2")
-            nc.scalar.activation(err2[:], t["near", q][:], ACT.Square, bias=consts[:, 1:2], scale=-1.0)
+        def make_series(q):
+            series[q] = per_quarter.tile([P, V], F32, name="series")
+            nc.scalar.activation(series[q][:], err2[q][:], ACT.Square, bias=bias_half, scale=1.0)
 
-        def g2b(q):
-            err2 = t["err2", q]
-            series = t["series", q] = ring.tile([P, V], F32, name="series")
-            nc.scalar.activation(series[:], err2[:], ACT.Square, bias=consts[:, 2:3], scale=1.0)
+        def make_quot0(q):
+            quot0[q] = per_quarter.tile([P, V], F32, name="quot0")
+            nc.vector.scalar_tensor_tensor(quot0[q][:], guess[q][:], GUESS_FLOOR, sum_p[q][:], ALU.add, ALU.mult)
 
-        def g2c(q):
-            quot1 = t["q1", q] = ring.tile([P, V], F32, name="quot1")
-            nc.vector.scalar_tensor_tensor(quot1[:], t["near", q][:], -2.0, t["q0", q][:], ALU.add, ALU.mult)
+        def make_quot1(q):
+            quot1[q] = per_quarter.tile([P, V], F32, name="quot1")
+            nc.vector.scalar_tensor_tensor(quot1[q][:], near_one[q][:], -2.0, quot0[q][:], ALU.add, ALU.mult)
 
-        def g3(q):
-            gap_t = t["gap_t", q] = gap_unit[q][:, V:]
-            nc.vector.scalar_tensor_tensor(gap_t, t["series", q][:], 0.75, t["q1", q][:], ALU.add, ALU.mult)
+        def make_gap(q):
+            nc.vector.scalar_tensor_tensor(gap_turned[q], series[q][:], 0.75, quot1[q][:], ALU.add, ALU.mult)
 
-        def g4(q):
-            gap = t["gap", q] = psum.tile([P, HALF], F32, name="bank")
+        def turn_gap_back(q):
+            gap[q] = psum.tile([P, V], F32, name="bank")
             for h in range(2):
-                turn(gap[:, P * h : P * h + P], t["gap_t", q][:, P * h : P * h + P])
+                turn(gap[q][:, P * h : P * (h + 1)], gap_turned[q][:, P * h : P * (h + 1)])
 
-        def g5(q):
-            gap = t["gap", q]
-            nc.vector.tensor_tensor(neg_ev[q][:, :V], gap[:, :V], best[q], ALU.subtract)
+        def fill_ev_window(q):
+            nc.vector.tensor_tensor(ev_window[q][:, :V], gap[q][:], best[q], ALU.subtract)
 
-        def g5b(q):
-            gap = t["gap", q]
-            nc.scalar.activation(gap_unit[q][:, :V], gap[:, :V], ACT.Copy, scale=half_unit[:, q : q + 1])
+        def fill_gap_window(q):
+            nc.scalar.activation(gap_window[q][:, :V], gap[q][:], ACT.Copy, scale=half_unit[:, q : q + 1])
 
-        def k0(q, rh):
-            picks = slot_sb[:, 16 * rh : 16 * rh + 16]
-            ev_slot = t["ev_slot", q, rh] = wide.tile([P, 256], F32, name="ev_slot")
-            nc.scalar.activation(ev_slot[:], neg_ev[q][:].indirect(picks), ACT.Copy)
+        def look_up_ev(q, s):
+            neg_ev_slot[q, s] = per_half.tile([P, SLOT_HALF], F32, name="neg_ev_slot")
+            picks = slot_sb[:, 16 * s : 16 * (s + 1)]
+            nc.scalar.activation(neg_ev_slot[q, s][:], ev_window[q][:].indirect(picks), ACT.Copy)
 
-        def k0b(q, rh):
-            picks = slot_sb[:, 16 * rh : 16 * rh + 16]
-            gap_slot = t["gap_slot", q, rh] = wide.tile([P, 256], F32, name="gap_slot")
-            if q >= 0:
-                nc.vector.tensor_copy(gap_slot[:], gap_unit[q][:].indirect(picks))
-            else:
-                nc.scalar.activation(gap_slot[:], gap_unit[q][:].indirect(picks), ACT.Copy)
+        def look_up_gap(q, s):
+            gap_slot[q, s] = per_half.tile([P, SLOT_HALF], F32, name="gap_slot")
+            picks = slot_sb[:, 16 * s : 16 * (s + 1)]
+            nc.vector.tensor_copy(gap_slot[q, s][:], gap_window[q][:].indirect(picks))
 
-        def k1(q, rh):
-            zg = t["zg", q, rh] = psum.tile([P, HALF], F32, name="bank")
+        def turn_slots(q, s):
+            turned[q, s] = psum.tile([P, 2, 2, P], F32, name="bank")
             for b in range(2):
-                cols = slice(P * b, P * b + P)
-                r0 = 256 * rh + P * b
-                turn(zg[:, cols], thr_sb[:, q, r0 : r0 + P], True, False)
-                turn(zg[:, cols], t["ev_slot", q, rh][:, cols], False, True)
+                first = SLOT_HALF * s + P * b
+                turn(turned[q, s][:, 0, b, :], thr_sb[:, q, first : first + P], True, False)
+                turn(turned[q, s][:, 0, b, :], neg_ev_slot[q, s][:, P * b : P * (b + 1)], False, True)
             for b in range(2):
-                turn(zg[:, 256 + P * b : 256 + P * b + P], t["gap_slot", q, rh][:, P * b : P * b + P])
+                turn(turned[q, s][:, 1, b, :], gap_slot[q, s][:, P * b : P * (b + 1)])
 
-        def k2(q, rh):
-            keepish = t["keepish", q, rh] = wide.tile([P, 256], F32, name="keepish")
-            nc.scalar.activation(keepish[:], t["zg", q, rh][:, :256], ACT.Tanh, scale=-1.0)
+        def make_tanh(q, s):
+            tanh_z[q, s] = per_half.tile([P, 2, P], F32, name="tanh_z")
+            nc.scalar.activation(tanh_z[q, s][:], turned[q, s][:, 0, :, :], ACT.Tanh, scale=-1.0)
 
-        def k3(q, rh):
+        def make_hid(q, s):
             nc.vector.scalar_tensor_tensor(
-                hid_t[rh][:, :, P * q : P * q + P],
-                t["keepish", q, rh][:].rearrange("p (b f) -> p b f", b=2),
-                1.0,
-                t["zg", q, rh][:, 256:].rearrange("p (b f) -> p b f", b=2),
-                ALU.add,
-                ALU.mult,
+                hid_turned[s][:, :, P * q : P * (q + 1)], tanh_z[q, s][:], 1.0, turned[q, s][:, 1, :, :], ALU.add, ALU.mult
             )
 
-        def e0(rb):
-            pairs = t["pairs", rb] = psum.tile([P, 2, P], F32, name="bank")
-            words = hid_t[rb // 2][:, rb % 2, :].bitcast(F32)
+        def turn_pairs(b):
+            pairs[b] = psum.tile([P, 2, P], F32, name="bank")
+            words = hid_turned[b // 2][:, b % 2, :].bitcast(F32)
             for u in range(2):
-                turn(pairs[:, u, :], words[:, u::2])
+                turn(pairs[b][:, u, :], words[:, u::2])
 
-        def e1(rb):
-            grouped = t["grouped", rb] = ring.tile([P, P * 4], BF16, name="grouped", align_bytes=64)
-            (nc.vector.tensor_copy if rb % 2 else nc.scalar.copy)(
-                grouped[:].bitcast(F32).rearrange("p (r u) -> p r u", u=2),
-                t["pairs", rb][:].rearrange("p u r -> p r u"),
-            )
+        def group_pairs(b):
+            grouped[b] = per_quarter.tile([P, 4 * P], BF16, name="grouped", align_bytes=64)
+            move = nc.vector.tensor_copy if b % 2 else nc.scalar.copy
+            move(grouped[b][:].bitcast(F32).rearrange("p (r u) -> p r u", u=2), pairs[b][:].rearrange("p u r -> p r u"))
 
-        def e2(rb):
-            codes = t["codes", rb] = ring.tile([P, P], U32, name="codes", align_bytes=64)
-            planes = t["planes", rb] = ring.tile([P, P], U8, name="planes", align_bytes=64)
-            nc.vector.quantize_mx(codes[:].bitcast(FP8X4), planes[:], t["grouped", rb][:])
+        def quantise(b):
+            hid_codes[b] = per_quarter.tile([P, P], U32, name="hid_codes", align_bytes=64)
+            hid_scale[b] = per_quarter.tile([P, P], U8, name="hid_scale", align_bytes=64)
+            nc.vector.quantize_mx(hid_codes[b][:].bitcast(FP8X4), hid_scale[b][:], grouped[b][:])
 
-        def e3(rb):
-            acc = t["acc", rb] = psum.tile([P, 2, P], F32, name="bank")
-            for mt in range(2):
+        def last_product(b):
+            acc[b] = psum.tile([P, N // P, P], F32, name="bank")
+            for m in range(N // P):
                 nc.tensor.matmul_mx(
-                    acc[:, mt, :],
-                    lhsT=w2w[:, 256 * mt : 256 * mt + 256].bitcast(FP4X4),
-                    lhsT_scale=w2s[:, P * mt : P * mt + P],
-                    rhs=t["codes", rb][:].bitcast(FP8X4),
-                    rhs_scale=t["planes", rb][:],
+                    acc[b][:, m, :],
+                    lhsT=w2_codes[:, 2 * P * m : 2 * P * (m + 1)].bitcast(FP4X4),
+                    lhsT_scale=w2_scale[:, P * m : P * (m + 1)],
+                    rhs=hid_codes[b][:].bitcast(FP8X4),
+                    rhs_scale=hid_scale[b][:],
                     start=True,
                     stop=True,
                 )
 
-        def e4(rb):
-            res = ring.tile([P, 2, P], F32, name="res")
-            (nc.scalar.copy)(res[:], t["acc", rb][:])
-            nc.sync.dma_start(out.rearrange("(m p) r -> p m r", p=P)[:, :, P * rb : P * rb + P], res[:])
+        def store(b):
+            result = per_quarter.tile([P, N // P, P], F32, name="result")
+            nc.scalar.copy(result[:], acc[b][:])
+            nc.sync.dma_start(out.rearrange("(m p) r -> p m r", p=P)[:, :, P * b : P * (b + 1)], result[:])
 
+        group_steps = (
+            (1, largest), (2, subtract_largest), (3, exponentiate), (4, sum_e_and_multiply), (5, sum_products),
+        )
+        quarter_steps = (
+            (5, make_guess), (6, make_near_one), (7, make_err2), (8, make_series), (7, make_quot0), (8, make_quot1),
+            (9, make_gap), (10, turn_gap_back), (11, fill_ev_window), (12, fill_gap_window),
+        )
+        slot_steps = ((12, look_up_ev), (13, look_up_gap), (14, turn_slots), (15, make_tanh), (16, make_hid))
         plan = []
         for q in range(QUARTERS):
             for h in range(2):
-                for k, step in enumerate((largest, shifted, weights, weighted, summed)):
-                    plan.append((SK * (2 * q + h) + 1 + k, len(plan), step, (q, h)))
-            for k, step in ((0, g0), (1, g1), (2, g2), (3, g2b), (2, g1b), (3, g2c), (4, g3), (5, g4), (6, g5), (7, g5b)):
-                plan.append((SK * (2 * q + 1) + 5 + k + (0.01 if k == 0 else 0), len(plan), step, (q,)))
-            for rh in range(2):
-                for k, step in enumerate((k0, k0b, k1, k2, k3)):
-                    plan.append((SK * (2 * q + 1 + 0.5 * rh) + 12.01 + k, len(plan), step, (q, rh)))
-        for rb in range(4):
-            for k, step in enumerate((e0, e1, e2, e3, e4)):
-                plan.append((SK * 7.5 + 0.1 * rb + 17.02 + k, len(plan), step, (rb,)))
-        for when, tie, step, args in sorted(plan, key=lambda e: e[:2]):
+                plan.extend((STEP * n + LAG * (2 * q + h), step, (q, h)) for n, step in group_steps)
+            plan.extend((STEP * n + LAG * (2 * q + 1), step, (q,)) for n, step in quarter_steps)
+            for s in range(2):
+                plan.extend((STEP * n + LAG * (2 * q + 1) + LAG // 2 * s, step, (q, s)) for n, step in slot_steps)
+        for place, step, args in sorted(plan, key=lambda entry: entry[0]):
             step(*args)
+
+        for step in (turn_pairs, group_pairs, quantise, last_product, store):
+            for b in range(SLOT_BLOCKS):
+                step(b)

from contextlib import ExitStack

import concourse.mybir as mybir
from concourse.masks import make_identity

K, T, S, D, N, H, V, U = 1024, 2048, 1024, 4, 256, 512, 256, 512
FLOPS = 2 * K * H * S + 2 * H * N * U

F32 = mybir.dt.float32
BF16 = mybir.dt.bfloat16
I32 = mybir.dt.int32
U32 = mybir.dt.uint32
U16 = mybir.dt.uint16
U8 = mybir.dt.uint8
FP8X4 = mybir.dt.float8_e4m3fn_x4
FP4X4 = mybir.dt.float4_e2m1fn_x4
ALU = mybir.AluOpType
ACT = mybir.ActivationFunctionType
AX = mybir.AxisListType

P = 128
PASSES = K // 512
QUADS = 4
QUARTERS = H // P
LIST_HALF = S // 2
SLOT_HALF = U // 2
SLOT_BLOCKS = U // P
ROWS_AT = 96

GUESS_SLOPE, GUESS_SHIFT, GUESS_FLOOR = -0.9609375, 0.6875, 0.2135

GPSIMD_QUARTERS = 3

STEP, LAG = 20, 14


def tile_picked_ymaskd_gap_p_kernel(
    tc, x_words, x_scales, w1_words, w1_scales, thr, unit, w2_words, w2_scales, offs, slot, out
):
    nc = tc.nc
    with ExitStack() as ctx:
        keep = ctx.enter_context(tc.tile_pool(name="keep", bufs=1))
        per_quarter = ctx.enter_context(tc.tile_pool(name="per_quarter", bufs=QUARTERS))
        per_half = ctx.enter_context(tc.tile_pool(name="per_half", bufs=2 * QUARTERS))
        psum = ctx.enter_context(tc.psum_pool(name="psum", bufs=8))

        offs_sb = keep.tile([P, S // 16], U16, name="offs_sb")
        nc.sync.dma_start(offs_sb[:], offs)

        x_rows = keep.tile([P, T], U8, name="x_rows", align_bytes=64)
        nc.sync.dma_start(x_rows[ROWS_AT:, :].bitcast(I32), x_scales.rearrange("o g c -> g o c").bitcast(I32))
        nc.vector.memset(x_rows[:ROWS_AT, :].bitcast(I32), 0)
        x_table = [keep.tile([P, T], U32, name="x_table%d" % o, align_bytes=64) for o in range(PASSES)]
        w1_codes = keep.tile([P, PASSES, 2 * H], U8, name="w1_codes", align_bytes=64)
        for o in range(PASSES):
            nc.sync.dma_start(x_table[o][:].bitcast(I32), x_words[o].rearrange("p n j -> p (n j)").bitcast(I32))
        nc.sync.dma_start(w1_codes[:].bitcast(I32), w1_words.rearrange("o p c -> p o c").bitcast(I32))

        w1_scale = keep.tile([P, PASSES, H], U8, name="w1_scale", align_bytes=64)
        nc.gpsimd.memset(w1_scale[:].bitcast(I32), 0)
        for quad in range(QUADS):
            nc.gpsimd.dma_start(
                w1_scale[32 * quad : 32 * quad + 4, :, :].bitcast(I32),
                w1_scales[:, 4 * quad : 4 * quad + 4, :].rearrange("o r c -> r o c").bitcast(I32),
            )
        x_scale = [keep.tile([P, PASSES, LIST_HALF], U8, name="x_scale%d" % h, align_bytes=64) for h in range(2)]
        for h in range(2):
            nc.vector.memset(x_scale[h][:].bitcast(I32), 0)

        ident = keep.tile([P, P], F32, name="ident")
        make_identity(nc, ident[:])
        biases = keep.tile([P, 3], F32, name="biases")
        for column, value in enumerate((GUESS_SHIFT, 1.0, 0.5)):
            nc.vector.memset(biases[:, column : column + 1], value)
        bias_shift, bias_one, bias_half = biases[:, 0:1], biases[:, 1:2], biases[:, 2:3]

        ev_window = [keep.tile([P, 2 * V], F32, name="ev_window%d" % q) for q in range(QUARTERS)]
        gap_window = [keep.tile([P, 2 * V], F32, name="gap_window%d" % q) for q in range(QUARTERS)]
        best = [ev_window[q][:, V:] for q in range(QUARTERS)]
        gap_turned = [gap_window[q][:, V:] for q in range(QUARTERS)]

        for h in range(2):
            picked_rows = keep.tile([P, LIST_HALF], U8, name="picked_rows%d" % h, align_bytes=64)
            nc.vector.tensor_copy(picked_rows[:], x_rows[:].indirect(offs_sb[:, 32 * h : 32 * h + 32]))
            for quad in range(QUADS):
                first = ROWS_AT + 8 * quad
                nc.scalar.dma_start(
                    x_scale[h][32 * quad : 32 * quad + 4, :, :].bitcast(I32),
                    picked_rows[first : first + 8, :].bitcast(I32),
                )

        slot_sb = keep.tile([P, U // 16], U16, name="slot_sb")
        nc.sync.dma_start(slot_sb[:], slot)

        x_codes = {}
        for o in range(PASSES):
            for h in range(2):
                x_codes[o, h] = keep.tile([P, LIST_HALF], U32, name="x_codes%d%d" % (o, h), align_bytes=64)
                nc.vector.tensor_copy(x_codes[o, h][:], x_table[o][:].indirect(offs_sb[:, 32 * h : 32 * h + 32]))

        hid_turned = [keep.tile([P, 2, H], BF16, name="hid_turned%d" % s, align_bytes=64) for s in range(2)]

        def turn(dst, src, start=True, stop=True):
            nc.tensor.matmul(dst, src, ident[:], start=start, stop=stop, is_transpose=True)

        y = {}
        for h in range(2):
            for q in range(QUARTERS):
                y[q, h] = psum.tile([P, LIST_HALF], F32, name="bank")
                for o in range(PASSES):
                    nc.tensor.matmul_mx(
                        y[q, h][:],
                        lhsT=w1_codes[:, o, 2 * P * q : 2 * P * (q + 1)].bitcast(FP4X4),
                        lhsT_scale=w1_scale[:, o, P * q : P * (q + 1)],
                        rhs=x_codes[o, h][:].bitcast(FP8X4),
                        rhs_scale=x_scale[h][:, o, :],
                        start=(o == 0),
                        stop=(o == PASSES - 1),
                    )

        thr_sb = keep.tile([P, QUARTERS, U], F32, name="thr_sb", tag="x_table1", align_bytes=64)
        nc.sync.dma_start(thr_sb[:], thr.rearrange("(q p) r -> p q r", p=P))
        w2_scale = keep.tile([P, N], U8, name="w2_scale", tag="x_codes00", align_bytes=64)
        nc.gpsimd.memset(w2_scale[:].bitcast(I32), 0)
        w2_codes = keep.tile([P, 2 * N], U8, name="w2_codes", tag="x_table0", align_bytes=64)
        nc.sync.dma_start(w2_codes[:].bitcast(I32), w2_words[0].bitcast(I32))
        for quad in range(QUADS):
            nc.sync.dma_start(
                w2_scale[32 * quad : 32 * quad + 4, :].bitcast(I32),
                w2_scales[0, 4 * quad : 4 * quad + 4, :].bitcast(I32),
            )
        unit_sb = keep.tile([P, QUARTERS], F32, name="unit_sb", tag="x_codes10", align_bytes=64)
        with nc.allow_non_contiguous_dma(reason="one value for each partition and quarter"):
            nc.sync.dma_start(unit_sb[:], unit.rearrange("(q p) o -> p (q o)", p=P))
        half_unit = keep.tile([P, QUARTERS], F32, name="half_unit")
        nc.scalar.activation(half_unit[:], unit_sb[:], ACT.Copy, scale=0.5)

        diff, e, prod, sum_e, sum_p = {}, {}, {}, {}, {}
        guess, near_one, err2, series, quot0, quot1, gap = {}, {}, {}, {}, {}, {}, {}
        neg_ev_slot, gap_slot, turned, tanh_z = {}, {}, {}, {}
        pairs, grouped, hid_codes, hid_scale, acc = {}, {}, {}, {}, {}

        def largest(q, h):
            members = y[q, h][:].rearrange("p (v d) -> p v d", d=D)
            nc.vector.tensor_reduce(best[q][:, P * h : P * (h + 1)], members, AX.X, ALU.max)

        def subtract_largest(q, h):
            diff[q, h] = per_half.tile([P, D, P], F32, name="diff")
            top = best[q][:, P * h : P * (h + 1)].unsqueeze(1).to_broadcast([P, D, P])
            nc.vector.tensor_tensor(diff[q, h][:], y[q, h][:].rearrange("p (v d) -> p d v", d=D), top, ALU.subtract)

        def exponentiate(q, h):
            e[q, h] = per_half.tile([P, D, P], F32, name="e")
            nc.scalar.activation(e[q, h][:], diff[q, h][:], ACT.Exp)

        def sum_e_and_multiply(q, h):
            if h == 0:
                sum_e[q] = psum.tile([P, V], F32, name="bank")
            for d in range(D):
                turn(sum_e[q][:, P * h : P * (h + 1)], e[q, h][:, d, :], d == 0, d == D - 1)
            prod[q, h] = per_half.tile([P, D, P], F32, name="prod")
            engine = nc.gpsimd if q < GPSIMD_QUARTERS else nc.vector
            engine.tensor_tensor(prod[q, h][:], e[q, h][:], diff[q, h][:], ALU.mult)

        def sum_products(q, h):
            if h == 0:
                sum_p[q] = psum.tile([P, V], F32, name="bank")
            for d in range(D):
                turn(sum_p[q][:, P * h : P * (h + 1)], prod[q, h][:, d, :], d == 0, d == D - 1)

        def make_guess(q):
            guess[q] = per_quarter.tile([P, V], F32, name="guess")
            nc.scalar.activation(guess[q][:], sum_e[q][:], ACT.Exp, bias=bias_shift, scale=GUESS_SLOPE)

        def make_near_one(q):
            near_one[q] = per_quarter.tile([P, V], F32, name="near_one")
            nc.vector.scalar_tensor_tensor(near_one[q][:], guess[q][:], GUESS_FLOOR, sum_e[q][:], ALU.add, ALU.mult)

        def make_err2(q):
            err2[q] = per_quarter.tile([P, V], F32, name="err2")
            nc.scalar.activation(err2[q][:], near_one[q][:], ACT.Square, bias=bias_one, scale=-1.0)

        def make_series(q):
            series[q] = per_quarter.tile([P, V], F32, name="series")
            nc.scalar.activation(series[q][:], err2[q][:], ACT.Square, bias=bias_half, scale=1.0)

        def make_quot0(q):
            quot0[q] = per_quarter.tile([P, V], F32, name="quot0")
            nc.vector.scalar_tensor_tensor(quot0[q][:], guess[q][:], GUESS_FLOOR, sum_p[q][:], ALU.add, ALU.mult)

        def make_quot1(q):
            quot1[q] = per_quarter.tile([P, V], F32, name="quot1")
            nc.vector.scalar_tensor_tensor(quot1[q][:], near_one[q][:], -2.0, quot0[q][:], ALU.add, ALU.mult)

        def make_gap(q):
            nc.vector.scalar_tensor_tensor(gap_turned[q], series[q][:], 0.75, quot1[q][:], ALU.add, ALU.mult)

        def turn_gap_back(q):
            gap[q] = psum.tile([P, V], F32, name="bank")
            for h in range(2):
                turn(gap[q][:, P * h : P * (h + 1)], gap_turned[q][:, P * h : P * (h + 1)])

        def fill_ev_window(q):
            nc.vector.tensor_tensor(ev_window[q][:, :V], gap[q][:], best[q], ALU.subtract)

        def fill_gap_window(q):
            nc.scalar.activation(gap_window[q][:, :V], gap[q][:], ACT.Copy, scale=half_unit[:, q : q + 1])

        def look_up_ev(q, s):
            neg_ev_slot[q, s] = per_half.tile([P, SLOT_HALF], F32, name="neg_ev_slot")
            picks = slot_sb[:, 16 * s : 16 * (s + 1)]
            nc.scalar.activation(neg_ev_slot[q, s][:], ev_window[q][:].indirect(picks), ACT.Copy)

        def look_up_gap(q, s):
            gap_slot[q, s] = per_half.tile([P, SLOT_HALF], F32, name="gap_slot")
            picks = slot_sb[:, 16 * s : 16 * (s + 1)]
            nc.vector.tensor_copy(gap_slot[q, s][:], gap_window[q][:].indirect(picks))

        def turn_slots(q, s):
            turned[q, s] = psum.tile([P, 2, 2, P], F32, name="bank")
            for b in range(2):
                first = SLOT_HALF * s + P * b
                turn(turned[q, s][:, 0, b, :], thr_sb[:, q, first : first + P], True, False)
                turn(turned[q, s][:, 0, b, :], neg_ev_slot[q, s][:, P * b : P * (b + 1)], False, True)
            for b in range(2):
                turn(turned[q, s][:, 1, b, :], gap_slot[q, s][:, P * b : P * (b + 1)])

        def make_tanh(q, s):
            tanh_z[q, s] = per_half.tile([P, 2, P], F32, name="tanh_z")
            nc.scalar.activation(tanh_z[q, s][:], turned[q, s][:, 0, :, :], ACT.Tanh, scale=-1.0)

        def make_hid(q, s):
            nc.vector.scalar_tensor_tensor(
                hid_turned[s][:, :, P * q : P * (q + 1)], tanh_z[q, s][:], 1.0, turned[q, s][:, 1, :, :], ALU.add, ALU.mult
            )

        def turn_pairs(b):
            pairs[b] = psum.tile([P, 2, P], F32, name="bank")
            words = hid_turned[b // 2][:, b % 2, :].bitcast(F32)
            for u in range(2):
                turn(pairs[b][:, u, :], words[:, u::2])

        def group_pairs(b):
            grouped[b] = per_quarter.tile([P, 4 * P], BF16, name="grouped", align_bytes=64)
            move = nc.vector.tensor_copy if b % 2 else nc.scalar.copy
            move(grouped[b][:].bitcast(F32).rearrange("p (r u) -> p r u", u=2), pairs[b][:].rearrange("p u r -> p r u"))

        def quantise(b):
            hid_codes[b] = per_quarter.tile([P, P], U32, name="hid_codes", align_bytes=64)
            hid_scale[b] = per_quarter.tile([P, P], U8, name="hid_scale", align_bytes=64)
            nc.vector.quantize_mx(hid_codes[b][:].bitcast(FP8X4), hid_scale[b][:], grouped[b][:])

        def last_product(b):
            acc[b] = psum.tile([P, N // P, P], F32, name="bank")
            for m in range(N // P):
                nc.tensor.matmul_mx(
                    acc[b][:, m, :],
                    lhsT=w2_codes[:, 2 * P * m : 2 * P * (m + 1)].bitcast(FP4X4),
                    lhsT_scale=w2_scale[:, P * m : P * (m + 1)],
                    rhs=hid_codes[b][:].bitcast(FP8X4),
                    rhs_scale=hid_scale[b][:],
                    start=True,
                    stop=True,
                )

        def store(b):
            result = per_quarter.tile([P, N // P, P], F32, name="result")
            nc.scalar.copy(result[:], acc[b][:])
            nc.sync.dma_start(out.rearrange("(m p) r -> p m r", p=P)[:, :, P * b : P * (b + 1)], result[:])

        group_steps = (
            (1, largest), (2, subtract_largest), (3, exponentiate), (4, sum_e_and_multiply), (5, sum_products),
        )
        quarter_steps = (
            (5, make_guess), (6, make_near_one), (7, make_err2), (8, make_series), (7, make_quot0), (8, make_quot1),
            (9, make_gap), (10, turn_gap_back), (11, fill_ev_window), (12, fill_gap_window),
        )
        slot_steps = ((12, look_up_ev), (13, look_up_gap), (14, turn_slots), (15, make_tanh), (16, make_hid))
        plan = []
        for q in range(QUARTERS):
            for h in range(2):
                plan.extend((STEP * n + LAG * (2 * q + h), step, (q, h)) for n, step in group_steps)
            plan.extend((STEP * n + LAG * (2 * q + 1), step, (q,)) for n, step in quarter_steps)
            for s in range(2):
                plan.extend((STEP * n + LAG * (2 * q + 1) + LAG // 2 * s, step, (q, s)) for n, step in slot_steps)
        for place, step, args in sorted(plan, key=lambda entry: entry[0]):
            step(*args)

        for step in (turn_pairs, group_pairs, quantise, last_product, store):
            for b in range(SLOT_BLOCKS):
                step(b)
